import numpy as np
import ml_dtypes


def mxq(x, axis, fmt="e4m3"):
    dtype, down = {"e4m3": (ml_dtypes.float8_e4m3fn, 7), "e5m2": (ml_dtypes.float8_e5m2, 14)}[fmt]
    v = np.moveaxis(np.asarray(x, np.float32).astype(ml_dtypes.bfloat16).astype(np.float64), axis, -1)
    blocks = v.reshape(v.shape[:-1] + (-1, 32))
    amax = np.abs(blocks).max(-1, keepdims=True)
    byte = np.maximum(np.where(amax > 0, np.frexp(amax)[1] - 1 + 127, 0) - down, 1)
    scale = np.exp2(byte - 127.0)
    codes = (blocks / scale).astype(np.float32).astype(dtype).astype(np.float64)
    return np.moveaxis((codes * scale).reshape(v.shape), -1, axis)


WIDE = False


def mx_kscale(k):
    if not WIDE:
        return np.ones(k)
    levels = np.array([10, -10, 5, -5, 0])
    if k % 512:
        return np.exp2(np.random.permutation(np.resize(levels, k // 32))).repeat(32)
    a = np.empty((k // 512, 16))
    for p in range(k // 512):
        a[p, :8] = np.random.permutation(np.resize(levels, 8))
        for g in range(8):
            far = levels[np.abs(levels - a[p, g]) >= 10]
            a[p, g + 8] = far[np.random.randint(len(far))]
    return np.exp2(a.ravel()).repeat(32)


def f64(x):
    return np.asarray(x).astype(np.float64)


def striped(idx):
    return np.tile(idx.reshape(-1, 16).T, (8, 1)).astype(np.uint16)


def unstriped(offs):
    return offs[:16].T.reshape(-1).astype(np.int64)


def pack_weight(w):
    k, n = w.shape
    w = f64(np.asarray(w, np.float32).astype(ml_dtypes.bfloat16)).reshape(k // 32, 32, n)
    amax = np.abs(w).max(1)
    byte = np.clip(np.where(amax > 0, np.frexp(amax)[1] - 1 + 127 - 7, 1), 1, 254)
    scaled = (w * np.exp2(127.0 - byte)[:, None, :]).reshape(k, n).astype(np.float32)
    words = np.ascontiguousarray(scaled.reshape(k // 512, 128, 4, n).transpose(0, 1, 3, 2)).astype(ml_dtypes.float8_e4m3fn).view(np.uint8)
    return words, np.ascontiguousarray(byte.astype(np.uint8).reshape(k // 512, 16, n))


def unpack_weight(words, scales):
    g, p, n, _ = words.shape
    vals = np.ascontiguousarray(words).view(ml_dtypes.float8_e4m3fn).astype(np.float64) * np.repeat(np.exp2(scales.astype(np.float64) - 127.0), 8, axis=1)[..., None]
    return vals.transpose(0, 1, 3, 2).reshape(g * 512, n)


K, T, D, S, V, N = 1024, 1024, 2, 512, 256, 256


def setup_inputs():
    n = np.random.standard_normal
    s = mx_kscale(K)[:, None]
    words, scales = pack_weight(n((K, N)) / np.sqrt(K) / s)
    return {
        "xT": (n((K, T)) * s).astype(np.float32),
        "w_words": words,
        "w_scales": scales,
        "b": (0.3 * n((N, 1))).astype(np.float32),
        "gate": np.tile(np.random.uniform(0.2, 1.0, (D, 1, V)) / np.sqrt(D), (1, N, 1)).astype(np.float32),
        "offs": striped(np.random.permutation(T)[:S]),
        "pos1": striped(np.random.permutation(S)[:V]),
        "pos2": striped(np.random.permutation(S)[:V]),
    }


def reference(xT, w_words, w_scales, b, gate, offs, pos1, pos2):
    w = unpack_weight(w_words, w_scales)
    idx = unstriped(offs)
    xq = mxq(f64(xT)[:, idx], 0, "e4m3")
    y = w.T @ xq
    y = y + f64(b)
    return sum(f64(gate[d]) * y[:, unstriped(p)] for d, p in enumerate((pos1, pos2)))

@@ -1,0 +1,152 @@
+from contextlib import ExitStack
+
+import concourse.mybir as mybir
+
+F32 = mybir.dt.float32
+BF16 = mybir.dt.bfloat16
+U32 = mybir.dt.uint32
+I32 = mybir.dt.int32
+U16 = mybir.dt.uint16
+U8 = mybir.dt.uint8
+FP8X4 = mybir.dt.float8_e4m3fn_x4
+MULT = mybir.AluOpType.mult
+ADD = mybir.AluOpType.add
+IDENTITY = mybir.ActivationFunctionType.Identity
+
+P = 128
+K, T, S, V, N, D = 1024, 1024, 512, 256, 256, 2
+PASSES = K // 512
+BLOCKS = N // P
+HALF = S // 2
+CUTS = (((0, 256), (256, 384), (384, S)), ((0, 256), (256, S)))
+
+FLOPS = 2 * K * S * N + 3 * N * V
+
+
+def tile_picked_sub_lin_bias_sub_e_kernel(tc, xT, w_words, w_scales, b, gate, offs, pos1, pos2, out):
+    nc = tc.nc
+    with ExitStack() as ctx:
+        held = ctx.enter_context(tc.tile_pool(name="held", bufs=1))
+        psum = ctx.enter_context(tc.psum_pool(name="psum", bufs=1))
+
+        offs_sb = held.tile([P, S // 16], U16, name="offs_sb")
+        pos_sb = [held.tile([P, V // 16], U16, name=f"pos_sb{d}") for d in range(D)]
+
+        raw = [[held.tile([P, 2, T], F32, name=f"raw{a}{u}") for u in range(2)] for a in range(PASSES)]
+        pairs = [[held.tile([P, T, 2], BF16, name=f"pairs{a}{u}", align_bytes=64) for u in range(2)] for a in range(PASSES)]
+        grouped = [held.tile([P, 4 * S], BF16, name=f"grouped{a}", align_bytes=64) for a in range(PASSES)]
+        codes = [held.tile([P, S], U32, name=f"codes{a}", align_bytes=64) for a in range(PASSES)]
+        scales = [held.tile([P, S], U8, name=f"scales{a}", align_bytes=64) for a in range(PASSES)]
+        w_codes = held.tile([P, PASSES, N], U32, name="w_codes", align_bytes=64)
+        w_sc = held.tile([P, N], U8, name="w_sc", align_bytes=64)
+        bias = held.tile([P, BLOCKS], F32, name="bias")
+        gates = held.tile([P, BLOCKS, D, V], F32, name="gates")
+        y = [held.tile([P, S], F32, name=f"y{c}") for c in range(BLOCKS)]
+
+        nc.vector.memset(w_sc[:].bitcast(I32), 0)
+        x_rows = xT.rearrange("(a p u e) t -> a u p e t", a=PASSES, u=2, e=2)
+        loads = ((0, 0, 0, T), (0, 1, 0, T), (1, 0, 0, 512), (1, 0, 512, T), (1, 1, 0, 512), (1, 1, 512, 768), (1, 1, 768, T))
+        for i, (a, u, t0, t1) in enumerate(loads):
+            nc.sync.dma_start(out=raw[a][u][:, :, t0:t1], in_=x_rows[a, u][:, :, t0:t1])
+            if i == 0:
+                nc.sync.dma_start(offs_sb[:], offs)
+            if i == 3:
+                nc.sync.dma_start(pos_sb[0][:], pos1)
+                nc.sync.dma_start(pos_sb[1][:], pos2)
+        nc.sync.dma_start(out=w_codes[:].bitcast(I32), in_=w_words.rearrange("a p n r -> p a (n r)").bitcast(I32))
+        for q in range(4):
+            nc.sync.dma_start(
+                out=w_sc[32 * q : 32 * q + 8, :].bitcast(I32),
+                in_=w_scales[:, 4 * q : 4 * q + 4, :].bitcast(I32),
+            )
+        gate_rows = gate.rearrange("d (c p) v -> c p d v", c=BLOCKS)
+        nc.sync.dma_start(out=gates[:, 0, :, :], in_=gate_rows[0])
+        nc.sync.dma_start(out=bias[:], in_=b.rearrange("(c p) o -> p (c o)", c=BLOCKS))
+        nc.sync.dma_start(out=gates[:, 1, :, :], in_=gate_rows[1])
+
+        acc = [[psum.tile([P, n1 - n0], F32, name=f"acc{c}{i}") for i, (n0, n1) in enumerate(CUTS[c])] for c in range(BLOCKS)]
+
+        def cast(engine, a, u, t0, t1):
+            dst = pairs[a][u][:, t0:t1, :]
+            src = raw[a][u][:, :, t0:t1].rearrange("p e t -> p t e")
+            if engine == "v":
+                nc.vector.tensor_copy(out=dst, in_=src)
+            else:
+                nc.scalar.copy(out=dst, in_=src)
+
+        def gather(a, u, h0, h1):
+            offsets = offs_sb[:] if h1 - h0 == S else offs_sb[:, h0 // 16 : h1 // 16]
+            window = pairs[a][u][:].rearrange("p t e -> p (t e)").bitcast(U32)
+            dst = grouped[a][:].bitcast(U32).rearrange("p (n u) -> p n u", u=2)[:, h0:h1, u]
+            nc.vector.tensor_copy(out=dst, in_=window.indirect(offsets))
+
+        def quantise(a, h0, h1):
+            nc.vector.quantize_mx(
+                out=codes[a][:, h0:h1].bitcast(FP8X4), scales=scales[a][:, h0:h1], in_=grouped[a][:, 4 * h0 : 4 * h1]
+            )
+
+        def multiply(a, c, i):
+            n0, n1 = CUTS[c][i]
+            nc.tensor.matmul_mx(
+                out=acc[c][i][:],
+                lhsT=w_codes[:, a, c * P : (c + 1) * P].bitcast(FP8X4),
+                lhsT_scale=w_sc[4 * a :, c * P : (c + 1) * P],
+                rhs=codes[a][:, n0:n1].bitcast(FP8X4),
+                rhs_scale=scales[a][:, n0:n1],
+                start=(a == 0),
+                stop=(a == PASSES - 1),
+            )
+
+        def add_bias(engine, c, i):
+            n0, n1 = CUTS[c][i]
+            dst = y[c][:, n0:n1]
+            if engine == "v":
+                nc.vector.tensor_scalar(dst, acc[c][i][:], bias[:, c : c + 1], None, ADD)
+            else:
+                nc.scalar.activation(dst, acc[c][i][:], IDENTITY, bias=bias[:, c : c + 1])
+
+        cast("s", 0, 0, 0, 416)
+        cast("v", 0, 0, 416, T)
+        gather(0, 0, 0, S)
+        cast("s", 0, 1, 0, 480)
+        cast("v", 0, 1, 480, T)
+        gather(0, 1, 0, S)
+        cast("s", 1, 0, 0, 512)
+        cast("s", 1, 0, 512, T)
+        quantise(0, 0, S)
+        gather(1, 0, 0, S)
+        for c in range(BLOCKS):
+            for i in range(len(CUTS[c])):
+                multiply(0, c, i)
+        cast("s", 1, 1, 0, 512)
+        cast("s", 1, 1, 512, 768)
+        cast("v", 1, 1, 768, T)
+        gather(1, 1, 0, HALF)
+        gather(1, 1, HALF, S)
+        for n0, n1 in CUTS[0]:
+            quantise(1, n0, n1)
+        multiply(1, 0, 0)
+        multiply(1, 0, 1)
+        multiply(1, 0, 2)
+        multiply(1, 1, 0)
+        multiply(1, 1, 1)
+        add_bias("s", 0, 0)
+        add_bias("s", 0, 1)
+        add_bias("v", 0, 2)
+        add_bias("s", 1, 0)
+        add_bias("s", 1, 1)
+
+        def look_up(c, d):
+            term = held.tile([P, V], F32, name=f"term{c}{d}")
+            nc.vector.tensor_tensor(term[:], y[c][:].indirect(pos_sb[d][:]), gates[:, c, d, :], MULT)
+            return term
+
+        def finish(c, terms):
+            result = held.tile([P, V], F32, name=f"result{c}")
+            nc.vector.tensor_tensor(result[:], terms[0][:], terms[1][:], ADD)
+            nc.sync.dma_start(out=out[c * P : (c + 1) * P, :], in_=result[:])
+
+        first = [look_up(0, 0), look_up(0, 1)]
+        second = [look_up(1, 0), look_up(1, 1)]
+        finish(0, first)
+        finish(1, second)

@@ -18,6 +18,20 @@ K, T, S, V, N, D = 1024, 1024, 512, 256, 256, 2
 PASSES = K // 512
 BLOCKS = N // P
 HALF = S // 2
+LOADS = (
+    (0, 0, 0, 512, 256),
+    (0, 0, 512, T, 176),
+    (0, 1, 0, 512, 512),
+    (0, 1, 512, T, 144),
+    (1, 0, 0, 512, 272),
+    (1, 0, 512, 768, 256),
+    (1, 0, 768, T, 256),
+    (1, 1, 0, 512, 272),
+    (1, 1, 512, 768, 256),
+    (1, 1, 768, T, 80),
+)
+HELD_BACK = -1
+POOLED = (4, 7,)
 CUTS = (((0, 256), (256, 384), (384, S)), ((0, 256), (256, S)))
 
 FLOPS = 2 * K * S * N + 3 * N * V
@@ -32,47 +46,49 @@ def tile_picked_sub_lin_bias_sub_e_kernel(tc, xT, w_words, w_scales, b, gate, of
         offs_sb = held.tile([P, S // 16], U16, name="offs_sb")
         pos_sb = [held.tile([P, V // 16], U16, name=f"pos_sb{d}") for d in range(D)]
 
-        raw = [[held.tile([P, 2, T], F32, name=f"raw{a}{u}") for u in range(2)] for a in range(PASSES)]
+        raw = [
+            held.tile([P, 2, t1 - t0], F32, name=f"raw{i}", tag=f"raw{i}", align_bytes=64) for i, (a, u, t0, t1, ns) in enumerate(LOADS)
+        ]
         pairs = [[held.tile([P, T, 2], BF16, name=f"pairs{a}{u}", align_bytes=64) for u in range(2)] for a in range(PASSES)]
         grouped = [held.tile([P, 4 * S], BF16, name=f"grouped{a}", align_bytes=64) for a in range(PASSES)]
         codes = [held.tile([P, S], U32, name=f"codes{a}", align_bytes=64) for a in range(PASSES)]
-        scales = [held.tile([P, S], U8, name=f"scales{a}", align_bytes=64) for a in range(PASSES)]
+        scales = {1: held.tile([P, S], U8, name="scales1", align_bytes=64)}
         w_codes = held.tile([P, PASSES, N], U32, name="w_codes", align_bytes=64)
         w_sc = held.tile([P, N], U8, name="w_sc", align_bytes=64)
         bias = held.tile([P, BLOCKS], F32, name="bias")
-        gates = held.tile([P, BLOCKS, D, V], F32, name="gates")
+        gates = held.tile([P, D, V], F32, name="gates")
         y = [held.tile([P, S], F32, name=f"y{c}") for c in range(BLOCKS)]
 
         nc.vector.memset(w_sc[:].bitcast(I32), 0)
         x_rows = xT.rearrange("(a p u e) t -> a u p e t", a=PASSES, u=2, e=2)
-        loads = ((0, 0, 0, T), (0, 1, 0, T), (1, 0, 0, 512), (1, 0, 512, T), (1, 1, 0, 512), (1, 1, 512, 768), (1, 1, 768, T))
-        for i, (a, u, t0, t1) in enumerate(loads):
-            nc.sync.dma_start(out=raw[a][u][:, :, t0:t1], in_=x_rows[a, u][:, :, t0:t1])
+        for i, (a, u, t0, t1, ns) in enumerate(LOADS):
+            nc.sync.dma_start(out=raw[i][:], in_=x_rows[a, u][:, :, t0:t1])
             if i == 0:
                 nc.sync.dma_start(offs_sb[:], offs)
-            if i == 3:
-                nc.sync.dma_start(pos_sb[0][:], pos1)
-                nc.sync.dma_start(pos_sb[1][:], pos2)
         nc.sync.dma_start(out=w_codes[:].bitcast(I32), in_=w_words.rearrange("a p n r -> p a (n r)").bitcast(I32))
         for q in range(4):
             nc.sync.dma_start(
                 out=w_sc[32 * q : 32 * q + 8, :].bitcast(I32),
                 in_=w_scales[:, 4 * q : 4 * q + 4, :].bitcast(I32),
             )
-        gate_rows = gate.rearrange("d (c p) v -> c p d v", c=BLOCKS)
-        nc.sync.dma_start(out=gates[:, 0, :, :], in_=gate_rows[0])
         nc.sync.dma_start(out=bias[:], in_=b.rearrange("(c p) o -> p (c o)", c=BLOCKS))
-        nc.sync.dma_start(out=gates[:, 1, :, :], in_=gate_rows[1])
+        nc.sync.dma_start(out=gates[:], in_=gate.rearrange("d m v -> m d v")[0:P])
+        nc.sync.dma_start(pos_sb[0][:], pos1)
+        nc.sync.dma_start(pos_sb[1][:], pos2)
 
         acc = [[psum.tile([P, n1 - n0], F32, name=f"acc{c}{i}") for i, (n0, n1) in enumerate(CUTS[c])] for c in range(BLOCKS)]
 
-        def cast(engine, a, u, t0, t1):
-            dst = pairs[a][u][:, t0:t1, :]
-            src = raw[a][u][:, :, t0:t1].rearrange("p e t -> p t e")
-            if engine == "v":
-                nc.vector.tensor_copy(out=dst, in_=src)
-            else:
-                nc.scalar.copy(out=dst, in_=src)
+        def cast(a, u):
+            for i, load in enumerate(LOADS):
+                if load[:2] == (a, u):
+                    t0, t1, ns = load[2:]
+                    src = raw[i][:].rearrange("p e t -> p t e")
+                    if ns > 0:
+                        nc.scalar.copy(out=pairs[a][u][:, t0 : t0 + ns, :], in_=src[:, 0:ns, :])
+                    if i in POOLED:
+                        nc.gpsimd.tensor_scalar(pairs[a][u][:, t0 + ns : t1, :], src[:, ns:, :], 1.0, 0.0, MULT, ADD)
+                    elif ns < t1 - t0:
+                        nc.vector.tensor_copy(out=pairs[a][u][:, t0 + ns : t1, :], in_=src[:, ns:, :])
 
         def gather(a, u, h0, h1):
             offsets = offs_sb[:] if h1 - h0 == S else offs_sb[:, h0 // 16 : h1 // 16]
@@ -105,22 +121,18 @@ def tile_picked_sub_lin_bias_sub_e_kernel(tc, xT, w_words, w_scales, b, gate, of
             else:
                 nc.scalar.activation(dst, acc[c][i][:], IDENTITY, bias=bias[:, c : c + 1])
 
-        cast("s", 0, 0, 0, 416)
-        cast("v", 0, 0, 416, T)
+        cast(0, 0)
         gather(0, 0, 0, S)
-        cast("s", 0, 1, 0, 480)
-        cast("v", 0, 1, 480, T)
+        cast(0, 1)
         gather(0, 1, 0, S)
-        cast("s", 1, 0, 0, 512)
-        cast("s", 1, 0, 512, T)
+        cast(1, 0)
+        scales[0] = held.tile([P, S], U8, name="scales0", tag="scales0", align_bytes=64)
         quantise(0, 0, S)
         gather(1, 0, 0, S)
         for c in range(BLOCKS):
             for i in range(len(CUTS[c])):
                 multiply(0, c, i)
-        cast("s", 1, 1, 0, 512)
-        cast("s", 1, 1, 512, 768)
-        cast("v", 1, 1, 768, T)
+        cast(1, 1)
         gather(1, 1, 0, HALF)
         gather(1, 1, HALF, S)
         for n0, n1 in CUTS[0]:
@@ -136,17 +148,26 @@ def tile_picked_sub_lin_bias_sub_e_kernel(tc, xT, w_words, w_scales, b, gate, of
         add_bias("s", 1, 0)
         add_bias("s", 1, 1)
 
-        def look_up(c, d):
-            term = held.tile([P, V], F32, name=f"term{c}{d}")
-            nc.vector.tensor_tensor(term[:], y[c][:].indirect(pos_sb[d][:]), gates[:, c, d, :], MULT)
-            return term
+        terms = [[held.tile([P, V], F32, name=f"term{c}{d}") for d in range(D)] for c in range(BLOCKS)]
+        results = [held.tile([P, V], F32, name=f"result{c}") for c in range(BLOCKS)]
 
-        def finish(c, terms):
-            result = held.tile([P, V], F32, name=f"result{c}")
-            nc.vector.tensor_tensor(result[:], terms[0][:], terms[1][:], ADD)
-            nc.sync.dma_start(out=out[c * P : (c + 1) * P, :], in_=result[:])
+        def look_up(c, d, v0, v1):
+            offsets = pos_sb[d][:] if v1 - v0 == V else pos_sb[d][:, v0 // 16 : v1 // 16]
+            nc.vector.tensor_tensor(terms[c][d][:, v0:v1], y[c][:].indirect(offsets), gates[:, d, v0:v1], MULT)
 
-        first = [look_up(0, 0), look_up(0, 1)]
-        second = [look_up(1, 0), look_up(1, 1)]
-        finish(0, first)
-        finish(1, second)
+        def add_terms(c, v0, v1):
+            nc.vector.tensor_tensor(results[c][:, v0:v1], terms[c][0][:, v0:v1], terms[c][1][:, v0:v1], ADD)
+
+        def store(c):
+            nc.sync.dma_start(out=out[c * P : (c + 1) * P, :], in_=results[c][:])
+
+        look_up(0, 0, 0, V)
+        look_up(0, 1, 0, V)
+        look_up(1, 0, 0, V)
+        add_terms(0, 0, V)
+        store(0)
+        look_up(1, 1, 0, 128)
+        look_up(1, 1, 128, V)
+        add_terms(1, 0, 128)
+        add_terms(1, 128, V)
+        store(1)

@@ -28,7 +28,7 @@ LOADS = (
     (1, 0, 768, T, 256),
     (1, 1, 0, 512, 272),
     (1, 1, 512, 768, 256),
-    (1, 1, 768, T, 80),
+    (1, 1, 768, T, 128),
 )
 HELD_BACK = -1
 POOLED = (4, 7,)
@@ -53,7 +53,7 @@ def tile_picked_sub_lin_bias_sub_e_kernel(tc, xT, w_words, w_scales, b, gate, of
         grouped = [held.tile([P, 4 * S], BF16, name=f"grouped{a}", align_bytes=64) for a in range(PASSES)]
         codes = [held.tile([P, S], U32, name=f"codes{a}", align_bytes=64) for a in range(PASSES)]
         scales = {1: held.tile([P, S], U8, name="scales1", align_bytes=64)}
-        w_codes = held.tile([P, PASSES, N], U32, name="w_codes", align_bytes=64)
+        w_codes = [held.tile([P, N], U32, name=f"w_codes{a}", align_bytes=64) for a in range(PASSES)]
         w_sc = held.tile([P, N], U8, name="w_sc", align_bytes=64)
         bias = held.tile([P, BLOCKS], F32, name="bias")
         gates = held.tile([P, D, V], F32, name="gates")
@@ -65,12 +65,13 @@ def tile_picked_sub_lin_bias_sub_e_kernel(tc, xT, w_words, w_scales, b, gate, of
             nc.sync.dma_start(out=raw[i][:], in_=x_rows[a, u][:, :, t0:t1])
             if i == 0:
                 nc.sync.dma_start(offs_sb[:], offs)
-        nc.sync.dma_start(out=w_codes[:].bitcast(I32), in_=w_words.rearrange("a p n r -> p a (n r)").bitcast(I32))
         for q in range(4):
             nc.sync.dma_start(
                 out=w_sc[32 * q : 32 * q + 8, :].bitcast(I32),
                 in_=w_scales[:, 4 * q : 4 * q + 4, :].bitcast(I32),
             )
+        for a in range(PASSES):
+            nc.sync.dma_start(out=w_codes[a][:].bitcast(I32), in_=w_words[a].rearrange("p n r -> p (n r)").bitcast(I32))
         nc.sync.dma_start(out=bias[:], in_=b.rearrange("(c p) o -> p (c o)", c=BLOCKS))
         nc.sync.dma_start(out=gates[:], in_=gate.rearrange("d m v -> m d v")[0:P])
         nc.sync.dma_start(pos_sb[0][:], pos1)
@@ -105,7 +106,7 @@ def tile_picked_sub_lin_bias_sub_e_kernel(tc, xT, w_words, w_scales, b, gate, of
             n0, n1 = CUTS[c][i]
             nc.tensor.matmul_mx(
                 out=acc[c][i][:],
-                lhsT=w_codes[:, a, c * P : (c + 1) * P].bitcast(FP8X4),
+                lhsT=w_codes[a][:, c * P : (c + 1) * P].bitcast(FP8X4),
                 lhsT_scale=w_sc[4 * a :, c * P : (c + 1) * P],
                 rhs=codes[a][:, n0:n1].bitcast(FP8X4),
                 rhs_scale=scales[a][:, n0:n1],
@@ -142,8 +143,8 @@ def tile_picked_sub_lin_bias_sub_e_kernel(tc, xT, w_words, w_scales, b, gate, of
         multiply(1, 0, 2)
         multiply(1, 1, 0)
         multiply(1, 1, 1)
-        add_bias("s", 0, 0)
-        add_bias("s", 0, 1)
+        add_bias("v", 0, 0)
+        add_bias("v", 0, 1)
         add_bias("v", 0, 2)
         add_bias("s", 1, 0)
         add_bias("s", 1, 1)
@@ -161,13 +162,9 @@ def tile_picked_sub_lin_bias_sub_e_kernel(tc, xT, w_words, w_scales, b, gate, of
         def store(c):
             nc.sync.dma_start(out=out[c * P : (c + 1) * P, :], in_=results[c][:])
 
-        look_up(0, 0, 0, V)
-        look_up(0, 1, 0, V)
-        look_up(1, 0, 0, V)
-        add_terms(0, 0, V)
-        store(0)
-        look_up(1, 1, 0, 128)
-        look_up(1, 1, 128, V)
-        add_terms(1, 0, 128)
-        add_terms(1, 128, V)
-        store(1)
+        for c in range(BLOCKS):
+            for d in range(D):
+                look_up(c, d, 0, V)
+        for c in range(BLOCKS):
+            add_terms(c, 0, V)
+            store(c)

@@ -22,16 +22,16 @@ LOADS = (
     (0, 0, 0, 512, 256),
     (0, 0, 512, T, 176),
     (0, 1, 0, 512, 512),
-    (0, 1, 512, T, 144),
+    (0, 1, 512, T, 176),
     (1, 0, 0, 512, 272),
     (1, 0, 512, 768, 256),
     (1, 0, 768, T, 256),
     (1, 1, 0, 512, 272),
     (1, 1, 512, 768, 256),
-    (1, 1, 768, T, 128),
+    (1, 1, 768, T, 144),
 )
 HELD_BACK = -1
-POOLED = (4, 7,)
+POOLED = (4, 7, 9,)
 CUTS = (((0, 256), (256, 384), (384, S)), ((0, 256), (256, S)))
 
 FLOPS = 2 * K * S * N + 3 * N * V
@@ -125,10 +125,12 @@ def tile_picked_sub_lin_bias_sub_e_kernel(tc, xT, w_words, w_scales, b, gate, of
         cast(0, 0)
         gather(0, 0, 0, S)
         cast(0, 1)
-        gather(0, 1, 0, S)
+        gather(0, 1, 0, HALF)
+        gather(0, 1, HALF, S)
         cast(1, 0)
         scales[0] = held.tile([P, S], U8, name="scales0", tag="scales0", align_bytes=64)
-        quantise(0, 0, S)
+        quantise(0, 0, HALF)
+        quantise(0, HALF, S)
         gather(1, 0, 0, S)
         for c in range(BLOCKS):
             for i in range(len(CUTS[c])):

@@ -11,6 +11,7 @@ U8 = mybir.dt.uint8
 FP8X4 = mybir.dt.float8_e4m3fn_x4
 MULT = mybir.AluOpType.mult
 ADD = mybir.AluOpType.add
+COPY = mybir.ActivationFunctionType.Copy
 IDENTITY = mybir.ActivationFunctionType.Identity
 
 P = 128
@@ -26,13 +27,12 @@ LOADS = (
     (1, 0, 0, 512, 272),
     (1, 0, 512, 768, 256),
     (1, 0, 768, T, 256),
-    (1, 1, 0, 512, 272),
-    (1, 1, 512, 768, 256),
-    (1, 1, 768, T, 144),
 )
-HELD_BACK = -1
-POOLED = (4, 7, 9,)
-CUTS = (((0, 256), (256, 384), (384, S)), ((0, 256), (256, S)))
+POOLED = (4,)
+ROWS = (2, 3)
+SPLIT = 192
+ROW_SHARE = {2: (256, 288), 3: (0, 192)}
+CUTS = (((256, 384), (0, 128), (128, 256), (384, S)), ((0, 256), (256, S)))
 
 FLOPS = 2 * K * S * N + 3 * N * V
 
@@ -49,15 +49,17 @@ def tile_picked_sub_lin_bias_sub_e_kernel(tc, xT, w_words, w_scales, b, gate, of
         raw = [
             held.tile([P, 2, t1 - t0], F32, name=f"raw{i}", tag=f"raw{i}", align_bytes=64) for i, (a, u, t0, t1, ns) in enumerate(LOADS)
         ]
-        pairs = [[held.tile([P, T, 2], BF16, name=f"pairs{a}{u}", align_bytes=64) for u in range(2)] for a in range(PASSES)]
+        pairs = [[held.tile([P, T, 2], BF16, name=f"pairs{a}{u}", align_bytes=64) for u in range(2 - a)] for a in range(PASSES)]
+        row_raw = {r: held.tile([P, T], F32, name=f"row_raw{r}", align_bytes=64) for r in ROWS}
+        row_bf = {r: held.tile([P, T], BF16, name=f"row_bf{r}", align_bytes=64) for r in ROWS}
         grouped = [held.tile([P, 4 * S], BF16, name=f"grouped{a}", align_bytes=64) for a in range(PASSES)]
         codes = [held.tile([P, S], U32, name=f"codes{a}", align_bytes=64) for a in range(PASSES)]
         scales = {1: held.tile([P, S], U8, name="scales1", align_bytes=64)}
-        w_codes = [held.tile([P, N], U32, name=f"w_codes{a}", align_bytes=64) for a in range(PASSES)]
+        w_codes = [held.tile([P, PASSES, P], U32, name=f"w_codes{c}", align_bytes=64) for c in range(BLOCKS)]
         w_sc = held.tile([P, N], U8, name="w_sc", align_bytes=64)
         bias = held.tile([P, BLOCKS], F32, name="bias")
         gates = held.tile([P, D, V], F32, name="gates")
-        y = [held.tile([P, S], F32, name=f"y{c}") for c in range(BLOCKS)]
+        y = [held.tile([P, S], F32, name=f"y{c}", tag=f"y{c}") for c in range(BLOCKS)]
 
         nc.vector.memset(w_sc[:].bitcast(I32), 0)
         x_rows = xT.rearrange("(a p u e) t -> a u p e t", a=PASSES, u=2, e=2)
@@ -65,14 +67,18 @@ def tile_picked_sub_lin_bias_sub_e_kernel(tc, xT, w_words, w_scales, b, gate, of
             nc.sync.dma_start(out=raw[i][:], in_=x_rows[a, u][:, :, t0:t1])
             if i == 0:
                 nc.sync.dma_start(offs_sb[:], offs)
+        for r in ROWS:
+            for t0 in (0, T // 2):
+                nc.sync.dma_start(out=row_raw[r][:, t0 : t0 + T // 2], in_=x_rows[1, 1][:, r - 2, t0 : t0 + T // 2])
         for q in range(4):
             nc.sync.dma_start(
                 out=w_sc[32 * q : 32 * q + 8, :].bitcast(I32),
                 in_=w_scales[:, 4 * q : 4 * q + 4, :].bitcast(I32),
             )
-        for a in range(PASSES):
-            nc.sync.dma_start(out=w_codes[a][:].bitcast(I32), in_=w_words[a].rearrange("p n r -> p (n r)").bitcast(I32))
+        w_view = w_words.rearrange("a p n r -> p a (n r)").bitcast(I32)
+        nc.sync.dma_start(out=w_codes[0][:].bitcast(I32), in_=w_view[:, :, 0:P])
         nc.sync.dma_start(out=bias[:], in_=b.rearrange("(c p) o -> p (c o)", c=BLOCKS))
+        nc.sync.dma_start(out=w_codes[1][:].bitcast(I32), in_=w_view[:, :, P:N])
         nc.sync.dma_start(out=gates[:], in_=gate.rearrange("d m v -> m d v")[0:P])
         nc.sync.dma_start(pos_sb[0][:], pos1)
         nc.sync.dma_start(pos_sb[1][:], pos2)
@@ -97,6 +103,21 @@ def tile_picked_sub_lin_bias_sub_e_kernel(tc, xT, w_words, w_scales, b, gate, of
             dst = grouped[a][:].bitcast(U32).rearrange("p (n u) -> p n u", u=2)[:, h0:h1, u]
             nc.vector.tensor_copy(out=dst, in_=window.indirect(offsets))
 
+        def round_row(r):
+            for t0, ns in zip((0, T // 2), ROW_SHARE[r]):
+                if ns > 0:
+                    nc.scalar.copy(out=row_bf[r][:, t0 : t0 + ns], in_=row_raw[r][:, t0 : t0 + ns])
+                rest = slice(t0 + ns, t0 + T // 2)
+                nc.gpsimd.tensor_scalar(row_bf[r][:, rest], row_raw[r][:, rest], 1.0, 0.0, MULT, ADD)
+
+        def gather_row(engine, r, h0, h1):
+            offsets = offs_sb[:, h0 // 16 : h1 // 16]
+            dst = grouped[1][:].rearrange("p (n j) -> p n j", j=4)[:, h0:h1, r]
+            if engine == "v":
+                nc.vector.tensor_copy(out=dst, in_=row_raw[r][:].indirect(offsets))
+            else:
+                nc.scalar.activation(dst, row_bf[r][:].indirect(offsets), COPY)
+
         def quantise(a, h0, h1):
             nc.vector.quantize_mx(
                 out=codes[a][:, h0:h1].bitcast(FP8X4), scales=scales[a][:, h0:h1], in_=grouped[a][:, 4 * h0 : 4 * h1]
@@ -106,7 +127,7 @@ def tile_picked_sub_lin_bias_sub_e_kernel(tc, xT, w_words, w_scales, b, gate, of
             n0, n1 = CUTS[c][i]
             nc.tensor.matmul_mx(
                 out=acc[c][i][:],
-                lhsT=w_codes[a][:, c * P : (c + 1) * P].bitcast(FP8X4),
+                lhsT=w_codes[c][:, a, :].bitcast(FP8X4),
                 lhsT_scale=w_sc[4 * a :, c * P : (c + 1) * P],
                 rhs=codes[a][:, n0:n1].bitcast(FP8X4),
                 rhs_scale=scales[a][:, n0:n1],
@@ -132,40 +153,49 @@ def tile_picked_sub_lin_bias_sub_e_kernel(tc, xT, w_words, w_scales, b, gate, of
         quantise(0, 0, HALF)
         quantise(0, HALF, S)
         gather(1, 0, 0, S)
-        for c in range(BLOCKS):
-            for i in range(len(CUTS[c])):
-                multiply(0, c, i)
-        cast(1, 1)
-        gather(1, 1, 0, HALF)
-        gather(1, 1, HALF, S)
+        for i in range(len(CUTS[0])):
+            multiply(0, 0, i)
+        round_row(2)
+        gather_row("s", 2, SPLIT, S)
+        gather_row("v", 2, 0, SPLIT)
+        round_row(3)
+        gather_row("v", 3, 0, SPLIT)
+        gather_row("s", 3, SPLIT, 384)
+        gather_row("s", 3, 384, S)
         for n0, n1 in CUTS[0]:
             quantise(1, n0, n1)
         multiply(1, 0, 0)
         multiply(1, 0, 1)
         multiply(1, 0, 2)
+        multiply(1, 0, 3)
+        multiply(0, 1, 0)
         multiply(1, 1, 0)
+        multiply(0, 1, 1)
         multiply(1, 1, 1)
         add_bias("v", 0, 0)
         add_bias("v", 0, 1)
-        add_bias("v", 0, 2)
+        add_bias("s", 0, 2)
+        add_bias("s", 0, 3)
         add_bias("s", 1, 0)
         add_bias("s", 1, 1)
 
-        terms = [[held.tile([P, V], F32, name=f"term{c}{d}") for d in range(D)] for c in range(BLOCKS)]
+        terms = {}
         results = [held.tile([P, V], F32, name=f"result{c}") for c in range(BLOCKS)]
 
         def look_up(c, d, v0, v1):
             offsets = pos_sb[d][:] if v1 - v0 == V else pos_sb[d][:, v0 // 16 : v1 // 16]
-            nc.vector.tensor_tensor(terms[c][d][:, v0:v1], y[c][:].indirect(offsets), gates[:, d, v0:v1], MULT)
+            nc.vector.tensor_tensor(terms[c, d][:, v0:v1], y[c][:].indirect(offsets), gates[:, d, v0:v1], MULT)
 
         def add_terms(c, v0, v1):
-            nc.vector.tensor_tensor(results[c][:, v0:v1], terms[c][0][:, v0:v1], terms[c][1][:, v0:v1], ADD)
+            nc.vector.tensor_tensor(results[c][:, v0:v1], terms[c, 0][:, v0:v1], terms[c, 1][:, v0:v1], ADD)
 
         def store(c):
             nc.sync.dma_start(out=out[c * P : (c + 1) * P, :], in_=results[c][:])
 
         for c in range(BLOCKS):
             for d in range(D):
+                tag = "y0" if (c, d) == (1, 0) else f"term{c}{d}"
+                terms[c, d] = held.tile([P, V], F32, name=f"term{c}{d}", tag=tag)
                 look_up(c, d, 0, V)
         for c in range(BLOCKS):
             add_terms(c, 0, V)

@@ -32,7 +32,7 @@ POOLED = (4,)
 ROWS = (2, 3)
 SPLIT = 192
 ROW_SHARE = {2: (256, 288), 3: (0, 192)}
-CUTS = (((256, 384), (0, 128), (128, 256), (384, S)), ((0, 256), (256, S)))
+CUTS = (((256, 384), (0, 128), (128, 256), (384, S)), ((0, S),))
 
 FLOPS = 2 * K * S * N + 3 * N * V
 
@@ -55,8 +55,8 @@ def tile_picked_sub_lin_bias_sub_e_kernel(tc, xT, w_words, w_scales, b, gate, of
         grouped = [held.tile([P, 4 * S], BF16, name=f"grouped{a}", align_bytes=64) for a in range(PASSES)]
         codes = [held.tile([P, S], U32, name=f"codes{a}", align_bytes=64) for a in range(PASSES)]
         scales = {1: held.tile([P, S], U8, name="scales1", align_bytes=64)}
-        w_codes = [held.tile([P, PASSES, P], U32, name=f"w_codes{c}", align_bytes=64) for c in range(BLOCKS)]
-        w_sc = held.tile([P, N], U8, name="w_sc", align_bytes=64)
+        w_codes = [held.tile([P, N], U32, name=f"w_codes{a}", align_bytes=64) for a in range(PASSES)]
+        w_sc = held.tile([P, PASSES, N], U8, name="w_sc", align_bytes=64)
         bias = held.tile([P, BLOCKS], F32, name="bias")
         gates = held.tile([P, D, V], F32, name="gates")
         y = [held.tile([P, S], F32, name=f"y{c}", tag=f"y{c}") for c in range(BLOCKS)]
@@ -70,15 +70,12 @@ def tile_picked_sub_lin_bias_sub_e_kernel(tc, xT, w_words, w_scales, b, gate, of
         for r in ROWS:
             for t0 in (0, T // 2):
                 nc.sync.dma_start(out=row_raw[r][:, t0 : t0 + T // 2], in_=x_rows[1, 1][:, r - 2, t0 : t0 + T // 2])
-        for q in range(4):
-            nc.sync.dma_start(
-                out=w_sc[32 * q : 32 * q + 8, :].bitcast(I32),
-                in_=w_scales[:, 4 * q : 4 * q + 4, :].bitcast(I32),
-            )
-        w_view = w_words.rearrange("a p n r -> p a (n r)").bitcast(I32)
-        nc.sync.dma_start(out=w_codes[0][:].bitcast(I32), in_=w_view[:, :, 0:P])
+        scale_rows = w_scales.rearrange("a (q r) n -> r q a n", r=4).bitcast(I32)
+        for r in range(4):
+            nc.sync.dma_start(out=w_sc[r:P:32, :, :].bitcast(I32), in_=scale_rows[r])
+        for a in range(PASSES):
+            nc.sync.dma_start(out=w_codes[a][:].bitcast(I32), in_=w_words[a].rearrange("p n r -> p (n r)").bitcast(I32))
         nc.sync.dma_start(out=bias[:], in_=b.rearrange("(c p) o -> p (c o)", c=BLOCKS))
-        nc.sync.dma_start(out=w_codes[1][:].bitcast(I32), in_=w_view[:, :, P:N])
         nc.sync.dma_start(out=gates[:], in_=gate.rearrange("d m v -> m d v")[0:P])
         nc.sync.dma_start(pos_sb[0][:], pos1)
         nc.sync.dma_start(pos_sb[1][:], pos2)
@@ -127,8 +124,8 @@ def tile_picked_sub_lin_bias_sub_e_kernel(tc, xT, w_words, w_scales, b, gate, of
             n0, n1 = CUTS[c][i]
             nc.tensor.matmul_mx(
                 out=acc[c][i][:],
-                lhsT=w_codes[c][:, a, :].bitcast(FP8X4),
-                lhsT_scale=w_sc[4 * a :, c * P : (c + 1) * P],
+                lhsT=w_codes[a][:, c * P : (c + 1) * P].bitcast(FP8X4),
+                lhsT_scale=w_sc[:, a, c * P : (c + 1) * P],
                 rhs=codes[a][:, n0:n1].bitcast(FP8X4),
                 rhs_scale=scales[a][:, n0:n1],
                 start=(a == 0),
@@ -155,6 +152,7 @@ def tile_picked_sub_lin_bias_sub_e_kernel(tc, xT, w_words, w_scales, b, gate, of
         gather(1, 0, 0, S)
         for i in range(len(CUTS[0])):
             multiply(0, 0, i)
+        multiply(0, 1, 0)
         round_row(2)
         gather_row("s", 2, SPLIT, S)
         gather_row("v", 2, 0, SPLIT)
@@ -168,35 +166,27 @@ def tile_picked_sub_lin_bias_sub_e_kernel(tc, xT, w_words, w_scales, b, gate, of
         multiply(1, 0, 1)
         multiply(1, 0, 2)
         multiply(1, 0, 3)
-        multiply(0, 1, 0)
         multiply(1, 1, 0)
-        multiply(0, 1, 1)
-        multiply(1, 1, 1)
         add_bias("v", 0, 0)
         add_bias("v", 0, 1)
         add_bias("s", 0, 2)
         add_bias("s", 0, 3)
         add_bias("s", 1, 0)
-        add_bias("s", 1, 1)
 
         terms = {}
-        results = [held.tile([P, V], F32, name=f"result{c}") for c in range(BLOCKS)]
 
-        def look_up(c, d, v0, v1):
-            offsets = pos_sb[d][:] if v1 - v0 == V else pos_sb[d][:, v0 // 16 : v1 // 16]
-            nc.vector.tensor_tensor(terms[c, d][:, v0:v1], y[c][:].indirect(offsets), gates[:, d, v0:v1], MULT)
+        def look_up(c, d, tag):
+            terms[c, d] = held.tile([P, V], F32, name=f"term{c}{d}", tag=tag)
+            nc.vector.tensor_tensor(terms[c, d][:], y[c][:].indirect(pos_sb[d][:]), gates[:, d, :], MULT)
 
-        def add_terms(c, v0, v1):
-            nc.vector.tensor_tensor(results[c][:, v0:v1], terms[c, 0][:, v0:v1], terms[c, 1][:, v0:v1], ADD)
+        def add_and_store(c, result):
+            nc.vector.tensor_tensor(result, terms[c, 0][:], terms[c, 1][:], ADD)
+            nc.sync.dma_start(out=out[c * P : (c + 1) * P, :], in_=result)
 
-        def store(c):
-            nc.sync.dma_start(out=out[c * P : (c + 1) * P, :], in_=results[c][:])
-
-        for c in range(BLOCKS):
-            for d in range(D):
-                tag = "y0" if (c, d) == (1, 0) else f"term{c}{d}"
-                terms[c, d] = held.tile([P, V], F32, name=f"term{c}{d}", tag=tag)
-                look_up(c, d, 0, V)
-        for c in range(BLOCKS):
-            add_terms(c, 0, V)
-            store(c)
+        look_up(0, 0, "term00")
+        look_up(0, 1, "term01")
+        look_up(1, 1, "term11")
+        look_up(1, 0, "y0")
+        add_and_store(0, gates[:, 1, :])
+        result = held.tile([P, V], F32, name="result")
+        add_and_store(1, result[:])

@@ -18,21 +18,23 @@ P = 128
 K, T, S, V, N, D = 1024, 1024, 512, 256, 256, 2
 PASSES = K // 512
 BLOCKS = N // P
-HALF = S // 2
-LOADS = (
-    (0, 0, 0, 512, 256),
-    (0, 0, 512, T, 176),
-    (0, 1, 0, 512, 512),
-    (0, 1, 512, T, 176),
-    (1, 0, 0, 512, 272),
-    (1, 0, 512, 768, 256),
-    (1, 0, 768, T, 256),
+HALF_LIST = S // 2
+HALF_ROW = T // 2
+LIST_ROWS = 16
+
+PAIR_LOADS = (
+    (0, 0, 0, 512, 256, "vector"),
+    (0, 0, 512, T, 176, "vector"),
+    (0, 1, 0, 512, 512, None),
+    (0, 1, 512, T, 176, "vector"),
+    (1, 0, 0, 512, 272, "gpsimd"),
+    (1, 0, 512, 768, 256, None),
+    (1, 0, 768, T, 256, None),
 )
-POOLED = (4,)
-ROWS = (2, 3)
+SCALAR_SHARE_OF_ROW = {2: HALF_ROW // 2, 3: 0}
 SPLIT = 192
-ROW_SHARE = {2: (256, 288), 3: (0, 192)}
-CUTS = (((256, 384), (0, 128), (128, 256), (384, S)), ((0, S),))
+LAST_PIECE = S - P
+PIECES = (((256, LAST_PIECE), (0, 128), (128, 256), (LAST_PIECE, S)), ((0, S),))
 
 FLOPS = 2 * K * S * N + 3 * N * V
 
@@ -43,15 +45,16 @@ def tile_picked_sub_lin_bias_sub_e_kernel(tc, xT, w_words, w_scales, b, gate, of
         held = ctx.enter_context(tc.tile_pool(name="held", bufs=1))
         psum = ctx.enter_context(tc.psum_pool(name="psum", bufs=1))
 
-        offs_sb = held.tile([P, S // 16], U16, name="offs_sb")
-        pos_sb = [held.tile([P, V // 16], U16, name=f"pos_sb{d}") for d in range(D)]
+        offs_sb = held.tile([P, S // LIST_ROWS], U16, name="offs_sb")
+        pos_sb = [held.tile([P, V // LIST_ROWS], U16, name=f"pos_sb{d}") for d in range(D)]
 
         raw = [
-            held.tile([P, 2, t1 - t0], F32, name=f"raw{i}", tag=f"raw{i}", align_bytes=64) for i, (a, u, t0, t1, ns) in enumerate(LOADS)
+            held.tile([P, 2, t1 - t0], F32, name=f"raw{i}", tag=f"raw{i}", align_bytes=64)
+            for i, (a, u, t0, t1, share, helper) in enumerate(PAIR_LOADS)
         ]
         pairs = [[held.tile([P, T, 2], BF16, name=f"pairs{a}{u}", align_bytes=64) for u in range(2 - a)] for a in range(PASSES)]
-        row_raw = {r: held.tile([P, T], F32, name=f"row_raw{r}", align_bytes=64) for r in ROWS}
-        row_bf = {r: held.tile([P, T], BF16, name=f"row_bf{r}", align_bytes=64) for r in ROWS}
+        row_raw = {j: held.tile([P, T], F32, name=f"row_raw{j}", align_bytes=64) for j in SCALAR_SHARE_OF_ROW}
+        row_bf = {j: held.tile([P, T], BF16, name=f"row_bf{j}", align_bytes=64) for j in SCALAR_SHARE_OF_ROW}
         grouped = [held.tile([P, 4 * S], BF16, name=f"grouped{a}", align_bytes=64) for a in range(PASSES)]
         codes = [held.tile([P, S], U32, name=f"codes{a}", align_bytes=64) for a in range(PASSES)]
         scales = {1: held.tile([P, S], U8, name="scales1", align_bytes=64)}
@@ -63,13 +66,13 @@ def tile_picked_sub_lin_bias_sub_e_kernel(tc, xT, w_words, w_scales, b, gate, of
 
         nc.vector.memset(w_sc[:].bitcast(I32), 0)
         x_rows = xT.rearrange("(a p u e) t -> a u p e t", a=PASSES, u=2, e=2)
-        for i, (a, u, t0, t1, ns) in enumerate(LOADS):
+        for i, (a, u, t0, t1, share, helper) in enumerate(PAIR_LOADS):
             nc.sync.dma_start(out=raw[i][:], in_=x_rows[a, u][:, :, t0:t1])
             if i == 0:
                 nc.sync.dma_start(offs_sb[:], offs)
-        for r in ROWS:
-            for t0 in (0, T // 2):
-                nc.sync.dma_start(out=row_raw[r][:, t0 : t0 + T // 2], in_=x_rows[1, 1][:, r - 2, t0 : t0 + T // 2])
+        for j in SCALAR_SHARE_OF_ROW:
+            for t0 in (0, HALF_ROW):
+                nc.sync.dma_start(out=row_raw[j][:, t0 : t0 + HALF_ROW], in_=x_rows[1, 1][:, j - 2, t0 : t0 + HALF_ROW])
         scale_rows = w_scales.rearrange("a (q r) n -> r q a n", r=4).bitcast(I32)
         for r in range(4):
             nc.sync.dma_start(out=w_sc[r:P:32, :, :].bitcast(I32), in_=scale_rows[r])
@@ -80,48 +83,54 @@ def tile_picked_sub_lin_bias_sub_e_kernel(tc, xT, w_words, w_scales, b, gate, of
         nc.sync.dma_start(pos_sb[0][:], pos1)
         nc.sync.dma_start(pos_sb[1][:], pos2)
 
-        acc = [[psum.tile([P, n1 - n0], F32, name=f"acc{c}{i}") for i, (n0, n1) in enumerate(CUTS[c])] for c in range(BLOCKS)]
+        acc = [[psum.tile([P, n1 - n0], F32, name=f"acc{c}{i}") for i, (n0, n1) in enumerate(PIECES[c])] for c in range(BLOCKS)]
 
-        def cast(a, u):
-            for i, load in enumerate(LOADS):
+        def round_on_gpsimd(dst, src):
+            nc.gpsimd.tensor_scalar(dst, src, 1.0, 0.0, MULT, ADD)
+
+        def round_pair(a, u):
+            for i, load in enumerate(PAIR_LOADS):
                 if load[:2] == (a, u):
-                    t0, t1, ns = load[2:]
+                    t0, t1, share, helper = load[2:]
                     src = raw[i][:].rearrange("p e t -> p t e")
-                    if ns > 0:
-                        nc.scalar.copy(out=pairs[a][u][:, t0 : t0 + ns, :], in_=src[:, 0:ns, :])
-                    if i in POOLED:
-                        nc.gpsimd.tensor_scalar(pairs[a][u][:, t0 + ns : t1, :], src[:, ns:, :], 1.0, 0.0, MULT, ADD)
-                    elif ns < t1 - t0:
-                        nc.vector.tensor_copy(out=pairs[a][u][:, t0 + ns : t1, :], in_=src[:, ns:, :])
+                    nc.scalar.copy(out=pairs[a][u][:, t0 : t0 + share, :], in_=src[:, 0:share, :])
+                    if helper == "gpsimd":
+                        round_on_gpsimd(pairs[a][u][:, t0 + share : t1, :], src[:, share:, :])
+                    elif helper == "vector":
+                        nc.vector.tensor_copy(out=pairs[a][u][:, t0 + share : t1, :], in_=src[:, share:, :])
 
-        def gather(a, u, h0, h1):
-            offsets = offs_sb[:] if h1 - h0 == S else offs_sb[:, h0 // 16 : h1 // 16]
+        def round_row(j):
+            share = SCALAR_SHARE_OF_ROW[j]
+            for t0 in (0, HALF_ROW):
+                if share > 0:
+                    nc.scalar.copy(out=row_bf[j][:, t0 : t0 + share], in_=row_raw[j][:, t0 : t0 + share])
+                rest = slice(t0 + share, t0 + HALF_ROW)
+                round_on_gpsimd(row_bf[j][:, rest], row_raw[j][:, rest])
+
+        def entries(n0, n1):
+            return offs_sb[:, n0 // LIST_ROWS : n1 // LIST_ROWS]
+
+        def gather_pair(a, u, n0, n1):
             window = pairs[a][u][:].rearrange("p t e -> p (t e)").bitcast(U32)
-            dst = grouped[a][:].bitcast(U32).rearrange("p (n u) -> p n u", u=2)[:, h0:h1, u]
-            nc.vector.tensor_copy(out=dst, in_=window.indirect(offsets))
+            dst = grouped[a][:].bitcast(U32).rearrange("p (n u) -> p n u", u=2)[:, n0:n1, u]
+            nc.vector.tensor_copy(out=dst, in_=window.indirect(entries(n0, n1)))
 
-        def round_row(r):
-            for t0, ns in zip((0, T // 2), ROW_SHARE[r]):
-                if ns > 0:
-                    nc.scalar.copy(out=row_bf[r][:, t0 : t0 + ns], in_=row_raw[r][:, t0 : t0 + ns])
-                rest = slice(t0 + ns, t0 + T // 2)
-                nc.gpsimd.tensor_scalar(row_bf[r][:, rest], row_raw[r][:, rest], 1.0, 0.0, MULT, ADD)
+        def row_slots(j, n0, n1):
+            return grouped[1][:].rearrange("p (n j) -> p n j", j=4)[:, n0:n1, j]
 
-        def gather_row(engine, r, h0, h1):
-            offsets = offs_sb[:, h0 // 16 : h1 // 16]
-            dst = grouped[1][:].rearrange("p (n j) -> p n j", j=4)[:, h0:h1, r]
-            if engine == "v":
-                nc.vector.tensor_copy(out=dst, in_=row_raw[r][:].indirect(offsets))
-            else:
-                nc.scalar.activation(dst, row_bf[r][:].indirect(offsets), COPY)
+        def gather_row_on_vector(j, n0, n1):
+            nc.vector.tensor_copy(out=row_slots(j, n0, n1), in_=row_raw[j][:].indirect(entries(n0, n1)))
 
-        def quantise(a, h0, h1):
+        def gather_row_on_scalar(j, n0, n1):
+            nc.scalar.activation(row_slots(j, n0, n1), row_bf[j][:].indirect(entries(n0, n1)), COPY)
+
+        def quantise(a, n0, n1):
             nc.vector.quantize_mx(
-                out=codes[a][:, h0:h1].bitcast(FP8X4), scales=scales[a][:, h0:h1], in_=grouped[a][:, 4 * h0 : 4 * h1]
+                out=codes[a][:, n0:n1].bitcast(FP8X4), scales=scales[a][:, n0:n1], in_=grouped[a][:, 4 * n0 : 4 * n1]
             )
 
         def multiply(a, c, i):
-            n0, n1 = CUTS[c][i]
+            n0, n1 = PIECES[c][i]
             nc.tensor.matmul_mx(
                 out=acc[c][i][:],
                 lhsT=w_codes[a][:, c * P : (c + 1) * P].bitcast(FP8X4),
@@ -132,46 +141,45 @@ def tile_picked_sub_lin_bias_sub_e_kernel(tc, xT, w_words, w_scales, b, gate, of
                 stop=(a == PASSES - 1),
             )
 
-        def add_bias(engine, c, i):
-            n0, n1 = CUTS[c][i]
-            dst = y[c][:, n0:n1]
-            if engine == "v":
-                nc.vector.tensor_scalar(dst, acc[c][i][:], bias[:, c : c + 1], None, ADD)
-            else:
-                nc.scalar.activation(dst, acc[c][i][:], IDENTITY, bias=bias[:, c : c + 1])
+        def multiply_pass(a):
+            for c in range(BLOCKS):
+                for i in range(len(PIECES[c])):
+                    multiply(a, c, i)
 
-        cast(0, 0)
-        gather(0, 0, 0, S)
-        cast(0, 1)
-        gather(0, 1, 0, HALF)
-        gather(0, 1, HALF, S)
-        cast(1, 0)
+        def add_bias_on_vector(c, i):
+            n0, n1 = PIECES[c][i]
+            nc.vector.tensor_scalar(y[c][:, n0:n1], acc[c][i][:], bias[:, c : c + 1], None, ADD)
+
+        def add_bias_on_scalar(c, i):
+            n0, n1 = PIECES[c][i]
+            nc.scalar.activation(y[c][:, n0:n1], acc[c][i][:], IDENTITY, bias=bias[:, c : c + 1])
+
+        round_pair(0, 0)
+        gather_pair(0, 0, 0, S)
+        round_pair(0, 1)
+        gather_pair(0, 1, 0, HALF_LIST)
+        gather_pair(0, 1, HALF_LIST, S)
+        round_pair(1, 0)
         scales[0] = held.tile([P, S], U8, name="scales0", tag="scales0", align_bytes=64)
-        quantise(0, 0, HALF)
-        quantise(0, HALF, S)
-        gather(1, 0, 0, S)
-        for i in range(len(CUTS[0])):
-            multiply(0, 0, i)
-        multiply(0, 1, 0)
+        quantise(0, 0, HALF_LIST)
+        quantise(0, HALF_LIST, S)
+        gather_pair(1, 0, 0, S)
+        multiply_pass(0)
         round_row(2)
-        gather_row("s", 2, SPLIT, S)
-        gather_row("v", 2, 0, SPLIT)
+        gather_row_on_scalar(2, SPLIT, S)
+        gather_row_on_vector(2, 0, SPLIT)
         round_row(3)
-        gather_row("v", 3, 0, SPLIT)
-        gather_row("s", 3, SPLIT, 384)
-        gather_row("s", 3, 384, S)
-        for n0, n1 in CUTS[0]:
+        gather_row_on_vector(3, 0, SPLIT)
+        gather_row_on_scalar(3, SPLIT, LAST_PIECE)
+        gather_row_on_scalar(3, LAST_PIECE, S)
+        for n0, n1 in PIECES[0]:
             quantise(1, n0, n1)
-        multiply(1, 0, 0)
-        multiply(1, 0, 1)
-        multiply(1, 0, 2)
-        multiply(1, 0, 3)
-        multiply(1, 1, 0)
-        add_bias("v", 0, 0)
-        add_bias("v", 0, 1)
-        add_bias("s", 0, 2)
-        add_bias("s", 0, 3)
-        add_bias("s", 1, 0)
+        multiply_pass(1)
+        add_bias_on_vector(0, 0)
+        add_bias_on_vector(0, 1)
+        add_bias_on_scalar(0, 2)
+        add_bias_on_scalar(0, 3)
+        add_bias_on_scalar(1, 0)
 
         terms = {}
 
@@ -188,5 +196,5 @@ def tile_picked_sub_lin_bias_sub_e_kernel(tc, xT, w_words, w_scales, b, gate, of
         look_up(1, 1, "term11")
         look_up(1, 0, "y0")
         add_and_store(0, gates[:, 1, :])
-        result = held.tile([P, V], F32, name="result")
-        add_and_store(1, result[:])
+        last_sum = held.tile([P, V], F32, name="last_sum")
+        add_and_store(1, last_sum[:])

@@ -17,24 +17,12 @@ IDENTITY = mybir.ActivationFunctionType.Identity
 P = 128
 K, T, S, V, N, D = 1024, 1024, 512, 256, 256, 2
 PASSES = K // 512
+ROWS = 4
 BLOCKS = N // P
-HALF_LIST = S // 2
-HALF_ROW = T // 2
 LIST_ROWS = 16
-
-PAIR_LOADS = (
-    (0, 0, 0, 512, 256, "vector"),
-    (0, 0, 512, T, 176, "vector"),
-    (0, 1, 0, 512, 512, None),
-    (0, 1, 512, T, 176, "vector"),
-    (1, 0, 0, 512, 272, "gpsimd"),
-    (1, 0, 512, 768, 256, None),
-    (1, 0, 768, T, 256, None),
-)
-SCALAR_SHARE_OF_ROW = {2: HALF_ROW // 2, 3: 0}
-SPLIT = 192
-LAST_PIECE = S - P
-PIECES = (((256, LAST_PIECE), (0, 128), (128, 256), (LAST_PIECE, S)), ((0, S),))
+SPLIT = 256
+PIECES = ((0, SPLIT), (SPLIT, SPLIT + P), (SPLIT + P, S))
+PRODUCTS = (PIECES, ((0, SPLIT), (SPLIT, S)))
 
 FLOPS = 2 * K * S * N + 3 * N * V
 
@@ -47,154 +35,107 @@ def tile_picked_sub_lin_bias_sub_e_kernel(tc, xT, w_words, w_scales, b, gate, of
 
         offs_sb = held.tile([P, S // LIST_ROWS], U16, name="offs_sb")
         pos_sb = [held.tile([P, V // LIST_ROWS], U16, name=f"pos_sb{d}") for d in range(D)]
-
-        raw = [
-            held.tile([P, 2, t1 - t0], F32, name=f"raw{i}", tag=f"raw{i}", align_bytes=64)
-            for i, (a, u, t0, t1, share, helper) in enumerate(PAIR_LOADS)
+        rows = [[held.tile([P, T], F32, name=f"row{a}{j}", align_bytes=64) for j in range(ROWS)] for a in range(PASSES)]
+        planes = [held.tile([P, ROWS, S - SPLIT], BF16, name=f"planes{a}", align_bytes=64) for a in range(PASSES)]
+        grouped = [
+            [held.tile([P, ROWS * (n1 - n0)], BF16, name=f"grouped{a}{i}", align_bytes=64) for i, (n0, n1) in enumerate(PIECES)]
+            for a in range(PASSES)
         ]
-        pairs = [[held.tile([P, T, 2], BF16, name=f"pairs{a}{u}", align_bytes=64) for u in range(2 - a)] for a in range(PASSES)]
-        row_raw = {j: held.tile([P, T], F32, name=f"row_raw{j}", align_bytes=64) for j in SCALAR_SHARE_OF_ROW}
-        row_bf = {j: held.tile([P, T], BF16, name=f"row_bf{j}", align_bytes=64) for j in SCALAR_SHARE_OF_ROW}
-        grouped = [held.tile([P, 4 * S], BF16, name=f"grouped{a}", align_bytes=64) for a in range(PASSES)]
         codes = [held.tile([P, S], U32, name=f"codes{a}", align_bytes=64) for a in range(PASSES)]
-        scales = {1: held.tile([P, S], U8, name="scales1", align_bytes=64)}
+        scales = [held.tile([P, S], U8, name=f"scales{a}", align_bytes=64) for a in range(PASSES)]
         w_codes = [held.tile([P, N], U32, name=f"w_codes{a}", align_bytes=64) for a in range(PASSES)]
         w_sc = held.tile([P, PASSES, N], U8, name="w_sc", align_bytes=64)
         bias = held.tile([P, BLOCKS], F32, name="bias")
         gates = held.tile([P, D, V], F32, name="gates")
-        y = [held.tile([P, S], F32, name=f"y{c}", tag=f"y{c}") for c in range(BLOCKS)]
+        y = [held.tile([P, S], F32, name=f"y{c}") for c in range(BLOCKS)]
 
         nc.vector.memset(w_sc[:].bitcast(I32), 0)
-        x_rows = xT.rearrange("(a p u e) t -> a u p e t", a=PASSES, u=2, e=2)
-        for i, (a, u, t0, t1, share, helper) in enumerate(PAIR_LOADS):
-            nc.sync.dma_start(out=raw[i][:], in_=x_rows[a, u][:, :, t0:t1])
-            if i == 0:
-                nc.sync.dma_start(offs_sb[:], offs)
-        for j in SCALAR_SHARE_OF_ROW:
-            for t0 in (0, HALF_ROW):
-                nc.sync.dma_start(out=row_raw[j][:, t0 : t0 + HALF_ROW], in_=x_rows[1, 1][:, j - 2, t0 : t0 + HALF_ROW])
+        x_rows = xT.rearrange("(a p j) t -> a j p t", a=PASSES, j=ROWS)
+        for a in range(PASSES):
+            for j in range(ROWS):
+                nc.sync.dma_start(out=rows[a][j][:], in_=x_rows[a, j])
+                if (a, j) == (0, 0):
+                    nc.sync.dma_start(offs_sb[:], offs)
         scale_rows = w_scales.rearrange("a (q r) n -> r q a n", r=4).bitcast(I32)
         for r in range(4):
             nc.sync.dma_start(out=w_sc[r:P:32, :, :].bitcast(I32), in_=scale_rows[r])
         for a in range(PASSES):
             nc.sync.dma_start(out=w_codes[a][:].bitcast(I32), in_=w_words[a].rearrange("p n r -> p (n r)").bitcast(I32))
         nc.sync.dma_start(out=bias[:], in_=b.rearrange("(c p) o -> p (c o)", c=BLOCKS))
-        nc.sync.dma_start(out=gates[:], in_=gate.rearrange("d m v -> m d v")[0:P])
         nc.sync.dma_start(pos_sb[0][:], pos1)
         nc.sync.dma_start(pos_sb[1][:], pos2)
+        nc.sync.dma_start(out=gates[:], in_=gate.rearrange("d m v -> m d v")[0:P])
 
-        acc = [[psum.tile([P, n1 - n0], F32, name=f"acc{c}{i}") for i, (n0, n1) in enumerate(PIECES[c])] for c in range(BLOCKS)]
-
-        def round_on_gpsimd(dst, src):
-            nc.gpsimd.tensor_scalar(dst, src, 1.0, 0.0, MULT, ADD)
-
-        def round_pair(a, u):
-            for i, load in enumerate(PAIR_LOADS):
-                if load[:2] == (a, u):
-                    t0, t1, share, helper = load[2:]
-                    src = raw[i][:].rearrange("p e t -> p t e")
-                    nc.scalar.copy(out=pairs[a][u][:, t0 : t0 + share, :], in_=src[:, 0:share, :])
-                    if helper == "gpsimd":
-                        round_on_gpsimd(pairs[a][u][:, t0 + share : t1, :], src[:, share:, :])
-                    elif helper == "vector":
-                        nc.vector.tensor_copy(out=pairs[a][u][:, t0 + share : t1, :], in_=src[:, share:, :])
-
-        def round_row(j):
-            share = SCALAR_SHARE_OF_ROW[j]
-            for t0 in (0, HALF_ROW):
-                if share > 0:
-                    nc.scalar.copy(out=row_bf[j][:, t0 : t0 + share], in_=row_raw[j][:, t0 : t0 + share])
-                rest = slice(t0 + share, t0 + HALF_ROW)
-                round_on_gpsimd(row_bf[j][:, rest], row_raw[j][:, rest])
+        acc = [[psum.tile([P, n1 - n0], F32, name=f"acc{c}{i}") for i, (n0, n1) in enumerate(PRODUCTS[c])] for c in range(BLOCKS)]
 
         def entries(n0, n1):
             return offs_sb[:, n0 // LIST_ROWS : n1 // LIST_ROWS]
 
-        def gather_pair(a, u, n0, n1):
-            window = pairs[a][u][:].rearrange("p t e -> p (t e)").bitcast(U32)
-            dst = grouped[a][:].bitcast(U32).rearrange("p (n u) -> p n u", u=2)[:, n0:n1, u]
-            nc.vector.tensor_copy(out=dst, in_=window.indirect(entries(n0, n1)))
+        def gather_on_vector(a, j):
+            dst = grouped[a][0][:].rearrange("p (n j) -> p n j", j=ROWS)[:, :, j]
+            nc.vector.tensor_copy(out=dst, in_=rows[a][j][:].indirect(entries(0, SPLIT)))
 
-        def row_slots(j, n0, n1):
-            return grouped[1][:].rearrange("p (n j) -> p n j", j=4)[:, n0:n1, j]
+        def gather_on_scalar(a, j, n0, n1):
+            nc.scalar.activation(planes[a][:, j, n0 - SPLIT : n1 - SPLIT], rows[a][j][:].indirect(entries(n0, n1)), COPY)
 
-        def gather_row_on_vector(j, n0, n1):
-            nc.vector.tensor_copy(out=row_slots(j, n0, n1), in_=row_raw[j][:].indirect(entries(n0, n1)))
+        def weave(a, i, copy):
+            n0, n1 = PIECES[i]
+            src = planes[a][:, :, n0 - SPLIT : n1 - SPLIT].rearrange("p j (c e) -> p c j e", e=4)
+            copy(out=grouped[a][i][:].rearrange("p (c e j) -> p c j e", e=4, j=ROWS), in_=src)
 
-        def gather_row_on_scalar(j, n0, n1):
-            nc.scalar.activation(row_slots(j, n0, n1), row_bf[j][:].indirect(entries(n0, n1)), COPY)
+        def quantise(a, i):
+            n0, n1 = PIECES[i]
+            nc.vector.quantize_mx(out=codes[a][:, n0:n1].bitcast(FP8X4), scales=scales[a][:, n0:n1], in_=grouped[a][i][:])
 
-        def quantise(a, n0, n1):
-            nc.vector.quantize_mx(
-                out=codes[a][:, n0:n1].bitcast(FP8X4), scales=scales[a][:, n0:n1], in_=grouped[a][:, 4 * n0 : 4 * n1]
-            )
+        def multiply(a, c):
+            for i, (n0, n1) in enumerate(PRODUCTS[c]):
+                nc.tensor.matmul_mx(
+                    out=acc[c][i][:],
+                    lhsT=w_codes[a][:, c * P : (c + 1) * P].bitcast(FP8X4),
+                    lhsT_scale=w_sc[:, a, c * P : (c + 1) * P],
+                    rhs=codes[a][:, n0:n1].bitcast(FP8X4),
+                    rhs_scale=scales[a][:, n0:n1],
+                    start=(a == 0),
+                    stop=(a == PASSES - 1),
+                )
 
-        def multiply(a, c, i):
-            n0, n1 = PIECES[c][i]
-            nc.tensor.matmul_mx(
-                out=acc[c][i][:],
-                lhsT=w_codes[a][:, c * P : (c + 1) * P].bitcast(FP8X4),
-                lhsT_scale=w_sc[:, a, c * P : (c + 1) * P],
-                rhs=codes[a][:, n0:n1].bitcast(FP8X4),
-                rhs_scale=scales[a][:, n0:n1],
-                start=(a == 0),
-                stop=(a == PASSES - 1),
-            )
+        for j in range(ROWS):
+            gather_on_vector(0, j)
+            gather_on_scalar(0, j, SPLIT, S)
+        weave(0, 1, nc.scalar.copy)
+        weave(0, 2, nc.scalar.copy)
+        gather_on_vector(1, 0)
+        gather_on_scalar(1, 0, SPLIT, S)
+        for i in range(len(PIECES)):
+            quantise(0, i)
+        for c in range(BLOCKS):
+            multiply(0, c)
+        for j in range(1, ROWS - 1):
+            gather_on_vector(1, j)
+            gather_on_scalar(1, j, SPLIT, S)
+        gather_on_vector(1, ROWS - 1)
+        gather_on_scalar(1, ROWS - 1, *PIECES[1])
+        gather_on_scalar(1, ROWS - 1, *PIECES[2])
+        weave(1, 1, nc.scalar.copy)
+        weave(1, 2, nc.vector.tensor_copy)
+        for i in range(len(PIECES)):
+            quantise(1, i)
+        for c in range(BLOCKS):
+            multiply(1, c)
+            for i, (n0, n1) in enumerate(PRODUCTS[c]):
+                nc.scalar.activation(y[c][:, n0:n1], acc[c][i][:], IDENTITY, bias=bias[:, c : c + 1])
 
-        def multiply_pass(a):
-            for c in range(BLOCKS):
-                for i in range(len(PIECES[c])):
-                    multiply(a, c, i)
+        terms = [held.tile([P, D, V], F32, name=f"terms{c}") for c in range(BLOCKS)]
+        picked = held.tile([P, V], F32, name="picked")
 
-        def add_bias_on_vector(c, i):
-            n0, n1 = PIECES[c][i]
-            nc.vector.tensor_scalar(y[c][:, n0:n1], acc[c][i][:], bias[:, c : c + 1], None, ADD)
+        def add_and_store(c):
+            result = held.tile([P, V], F32, name=f"result{c}")
+            nc.vector.tensor_tensor(result[:], terms[c][:, 0, :], terms[c][:, 1, :], ADD)
+            nc.sync.dma_start(out=out[c * P : (c + 1) * P, :], in_=result[:])
 
-        def add_bias_on_scalar(c, i):
-            n0, n1 = PIECES[c][i]
-            nc.scalar.activation(y[c][:, n0:n1], acc[c][i][:], IDENTITY, bias=bias[:, c : c + 1])
-
-        round_pair(0, 0)
-        gather_pair(0, 0, 0, S)
-        round_pair(0, 1)
-        gather_pair(0, 1, 0, HALF_LIST)
-        gather_pair(0, 1, HALF_LIST, S)
-        round_pair(1, 0)
-        scales[0] = held.tile([P, S], U8, name="scales0", tag="scales0", align_bytes=64)
-        quantise(0, 0, HALF_LIST)
-        quantise(0, HALF_LIST, S)
-        gather_pair(1, 0, 0, S)
-        multiply_pass(0)
-        round_row(2)
-        gather_row_on_scalar(2, SPLIT, S)
-        gather_row_on_vector(2, 0, SPLIT)
-        round_row(3)
-        gather_row_on_vector(3, 0, SPLIT)
-        gather_row_on_scalar(3, SPLIT, LAST_PIECE)
-        gather_row_on_scalar(3, LAST_PIECE, S)
-        for n0, n1 in PIECES[0]:
-            quantise(1, n0, n1)
-        multiply_pass(1)
-        add_bias_on_vector(0, 0)
-        add_bias_on_vector(0, 1)
-        add_bias_on_scalar(0, 2)
-        add_bias_on_scalar(0, 3)
-        add_bias_on_scalar(1, 0)
-
-        terms = {}
-
-        def look_up(c, d, tag):
-            terms[c, d] = held.tile([P, V], F32, name=f"term{c}{d}", tag=tag)
-            nc.vector.tensor_tensor(terms[c, d][:], y[c][:].indirect(pos_sb[d][:]), gates[:, d, :], MULT)
-
-        def add_and_store(c, result):
-            nc.vector.tensor_tensor(result, terms[c, 0][:], terms[c, 1][:], ADD)
-            nc.sync.dma_start(out=out[c * P : (c + 1) * P, :], in_=result)
-
-        look_up(0, 0, "term00")
-        look_up(0, 1, "term01")
-        look_up(1, 1, "term11")
-        look_up(1, 0, "y0")
-        add_and_store(0, gates[:, 1, :])
-        last_sum = held.tile([P, V], F32, name="last_sum")
-        add_and_store(1, last_sum[:])
+        for c, d in ((0, 0), (0, 1), (1, 0)):
+            nc.vector.tensor_tensor(terms[c][:, d, :], y[c][:].indirect(pos_sb[d][:]), gates[:, d, :], MULT)
+        nc.scalar.activation(picked[:], y[1][:].indirect(pos_sb[1][:]), COPY)
+        nc.vector.tensor_tensor(terms[1][:, 1, :], picked[:], gates[:, 1, :], MULT)
+        add_and_store(0)
+        add_and_store(1)

@@ -44,23 +44,23 @@ def tile_picked_sub_lin_bias_sub_e_kernel(tc, xT, w_words, w_scales, b, gate, of
         codes = [held.tile([P, S], U32, name=f"codes{a}", align_bytes=64) for a in range(PASSES)]
         scales = [held.tile([P, S], U8, name=f"scales{a}", align_bytes=64) for a in range(PASSES)]
         w_codes = [held.tile([P, N], U32, name=f"w_codes{a}", align_bytes=64) for a in range(PASSES)]
-        w_sc = held.tile([P, PASSES, N], U8, name="w_sc", align_bytes=64)
         bias = held.tile([P, BLOCKS], F32, name="bias")
         gates = held.tile([P, D, V], F32, name="gates")
         y = [held.tile([P, S], F32, name=f"y{c}") for c in range(BLOCKS)]
 
-        nc.vector.memset(w_sc[:].bitcast(I32), 0)
+        scale_rows = w_scales.rearrange("a (q r) n -> q a r n", r=4).bitcast(I32)
         x_rows = xT.rearrange("(a p j) t -> a j p t", a=PASSES, j=ROWS)
         for a in range(PASSES):
             for j in range(ROWS):
                 nc.sync.dma_start(out=rows[a][j][:], in_=x_rows[a, j])
                 if (a, j) == (0, 0):
                     nc.sync.dma_start(offs_sb[:], offs)
-        scale_rows = w_scales.rearrange("a (q r) n -> r q a n", r=4).bitcast(I32)
-        for r in range(4):
-            nc.sync.dma_start(out=w_sc[r:P:32, :, :].bitcast(I32), in_=scale_rows[r])
-        for a in range(PASSES):
-            nc.sync.dma_start(out=w_codes[a][:].bitcast(I32), in_=w_words[a].rearrange("p n r -> p (n r)").bitcast(I32))
+                    for q in range(4):
+                        rows_q = scales[0][32 * q + 4 : 32 * q + 4 + 4 * PASSES, 0:N]
+                        nc.scalar.dma_start(out=rows_q.bitcast(I32), in_=scale_rows[q])
+        words = w_words.rearrange("a p n r -> a p (n r)").bitcast(I32)
+        for a, m0, m1 in ((0, 0, P), (0, P, N), (1, 0, N)):
+            nc.sync.dma_start(out=w_codes[a][:, m0:m1].bitcast(I32), in_=words[a][:, m0:m1])
         nc.sync.dma_start(out=bias[:], in_=b.rearrange("(c p) o -> p (c o)", c=BLOCKS))
         nc.sync.dma_start(pos_sb[0][:], pos1)
         nc.sync.dma_start(pos_sb[1][:], pos2)
@@ -92,7 +92,7 @@ def tile_picked_sub_lin_bias_sub_e_kernel(tc, xT, w_words, w_scales, b, gate, of
                 nc.tensor.matmul_mx(
                     out=acc[c][i][:],
                     lhsT=w_codes[a][:, c * P : (c + 1) * P].bitcast(FP8X4),
-                    lhsT_scale=w_sc[:, a, c * P : (c + 1) * P],
+                    lhsT_scale=scales[0][4 + 4 * a :, c * P : (c + 1) * P],
                     rhs=codes[a][:, n0:n1].bitcast(FP8X4),
                     rhs_scale=scales[a][:, n0:n1],
                     start=(a == 0),
@@ -123,7 +123,10 @@ def tile_picked_sub_lin_bias_sub_e_kernel(tc, xT, w_words, w_scales, b, gate, of
         for c in range(BLOCKS):
             multiply(1, c)
             for i, (n0, n1) in enumerate(PRODUCTS[c]):
-                nc.scalar.activation(y[c][:, n0:n1], acc[c][i][:], IDENTITY, bias=bias[:, c : c + 1])
+                if (c, i) == (0, 0):
+                    nc.vector.tensor_scalar(y[c][:, n0:n1], acc[c][i][:], bias[:, c : c + 1], None, ADD)
+                else:
+                    nc.scalar.activation(y[c][:, n0:n1], acc[c][i][:], IDENTITY, bias=bias[:, c : c + 1])
 
         terms = [held.tile([P, D, V], F32, name=f"terms{c}") for c in range(BLOCKS)]
         picked = held.tile([P, V], F32, name="picked")

@@ -21,8 +21,7 @@ ROWS = 4
 BLOCKS = N // P
 LIST_ROWS = 16
 SPLIT = 256
-PIECES = ((0, SPLIT), (SPLIT, SPLIT + P), (SPLIT + P, S))
-PRODUCTS = (PIECES, ((0, SPLIT), (SPLIT, S)))
+PIECES = S // P
 
 FLOPS = 2 * K * S * N + 3 * N * V
 
@@ -37,10 +36,7 @@ def tile_picked_sub_lin_bias_sub_e_kernel(tc, xT, w_words, w_scales, b, gate, of
         pos_sb = [held.tile([P, V // LIST_ROWS], U16, name=f"pos_sb{d}") for d in range(D)]
         rows = [[held.tile([P, T], F32, name=f"row{a}{j}", align_bytes=64) for j in range(ROWS)] for a in range(PASSES)]
         planes = [held.tile([P, ROWS, S - SPLIT], BF16, name=f"planes{a}", align_bytes=64) for a in range(PASSES)]
-        grouped = [
-            [held.tile([P, ROWS * (n1 - n0)], BF16, name=f"grouped{a}{i}", align_bytes=64) for i, (n0, n1) in enumerate(PIECES)]
-            for a in range(PASSES)
-        ]
+        grouped = [held.tile([P, ROWS * S], BF16, name=f"grouped{a}", align_bytes=64) for a in range(PASSES)]
         codes = [held.tile([P, S], U32, name=f"codes{a}", align_bytes=64) for a in range(PASSES)]
         scales = [held.tile([P, S], U8, name=f"scales{a}", align_bytes=64) for a in range(PASSES)]
         w_codes = [held.tile([P, N], U32, name=f"w_codes{a}", align_bytes=64) for a in range(PASSES)]
@@ -66,79 +62,79 @@ def tile_picked_sub_lin_bias_sub_e_kernel(tc, xT, w_words, w_scales, b, gate, of
         nc.sync.dma_start(pos_sb[1][:], pos2)
         nc.sync.dma_start(out=gates[:], in_=gate.rearrange("d m v -> m d v")[0:P])
 
-        acc = [[psum.tile([P, n1 - n0], F32, name=f"acc{c}{i}") for i, (n0, n1) in enumerate(PRODUCTS[c])] for c in range(BLOCKS)]
+        acc = [[psum.tile([P, P], F32, name=f"acc{c}{i}") for i in range(PIECES)] for c in range(BLOCKS)]
 
         def entries(n0, n1):
             return offs_sb[:, n0 // LIST_ROWS : n1 // LIST_ROWS]
 
-        def gather_on_vector(a, j):
-            dst = grouped[a][0][:].rearrange("p (n j) -> p n j", j=ROWS)[:, :, j]
-            nc.vector.tensor_copy(out=dst, in_=rows[a][j][:].indirect(entries(0, SPLIT)))
+        def gather_on_vector(a, j, n0, n1):
+            dst = grouped[a][:].rearrange("p (n j) -> p n j", j=ROWS)[:, n0:n1, j]
+            nc.vector.tensor_copy(out=dst, in_=rows[a][j][:].indirect(entries(n0, n1)))
 
         def gather_on_scalar(a, j, n0, n1):
             nc.scalar.activation(planes[a][:, j, n0 - SPLIT : n1 - SPLIT], rows[a][j][:].indirect(entries(n0, n1)), COPY)
 
-        def weave(a, i, copy):
-            n0, n1 = PIECES[i]
+        def weave(a, n0, n1, copy):
             src = planes[a][:, :, n0 - SPLIT : n1 - SPLIT].rearrange("p j (c e) -> p c j e", e=4)
-            copy(out=grouped[a][i][:].rearrange("p (c e j) -> p c j e", e=4, j=ROWS), in_=src)
+            copy(out=grouped[a][:, ROWS * n0 : ROWS * n1].rearrange("p (c e j) -> p c j e", e=4, j=ROWS), in_=src)
 
-        def quantise(a, i):
-            n0, n1 = PIECES[i]
-            nc.vector.quantize_mx(out=codes[a][:, n0:n1].bitcast(FP8X4), scales=scales[a][:, n0:n1], in_=grouped[a][i][:])
+        def quantise(a, n0, n1):
+            nc.vector.quantize_mx(
+                out=codes[a][:, n0:n1].bitcast(FP8X4), scales=scales[a][:, n0:n1], in_=grouped[a][:, ROWS * n0 : ROWS * n1]
+            )
 
-        def multiply(a, c):
-            for i, (n0, n1) in enumerate(PRODUCTS[c]):
-                nc.tensor.matmul_mx(
-                    out=acc[c][i][:],
-                    lhsT=w_codes[a][:, c * P : (c + 1) * P].bitcast(FP8X4),
-                    lhsT_scale=scales[0][4 + 4 * a :, c * P : (c + 1) * P],
-                    rhs=codes[a][:, n0:n1].bitcast(FP8X4),
-                    rhs_scale=scales[a][:, n0:n1],
-                    start=(a == 0),
-                    stop=(a == PASSES - 1),
-                )
+        def multiply(a, c, i):
+            nc.tensor.matmul_mx(
+                out=acc[c][i][:],
+                lhsT=w_codes[a][:, c * P : (c + 1) * P].bitcast(FP8X4),
+                lhsT_scale=scales[0][4 + 4 * a :, c * P : (c + 1) * P],
+                rhs=codes[a][:, i * P : (i + 1) * P].bitcast(FP8X4),
+                rhs_scale=scales[a][:, i * P : (i + 1) * P],
+                start=(a == 0),
+                stop=(a == PASSES - 1),
+            )
+
+        def add_bias(c, i):
+            dst = y[c][:, i * P : (i + 1) * P]
+            if c == 0:
+                nc.scalar.activation(dst, acc[c][i][:], IDENTITY, bias=bias[:, c : c + 1])
+            else:
+                nc.vector.tensor_scalar(dst, acc[c][i][:], bias[:, c : c + 1], None, ADD)
 
         for j in range(ROWS):
-            gather_on_vector(0, j)
+            gather_on_vector(0, j, 0, SPLIT)
             gather_on_scalar(0, j, SPLIT, S)
-        weave(0, 1, nc.scalar.copy)
-        weave(0, 2, nc.scalar.copy)
-        gather_on_vector(1, 0)
+        weave(0, SPLIT, S, nc.scalar.copy)
+        gather_on_vector(1, 0, 0, SPLIT)
         gather_on_scalar(1, 0, SPLIT, S)
-        for i in range(len(PIECES)):
-            quantise(0, i)
+        quantise(0, 0, SPLIT)
+        quantise(0, SPLIT, S)
         for c in range(BLOCKS):
-            multiply(0, c)
+            for i in range(PIECES):
+                multiply(0, c, i)
         for j in range(1, ROWS - 1):
-            gather_on_vector(1, j)
+            gather_on_vector(1, j, 0, SPLIT)
             gather_on_scalar(1, j, SPLIT, S)
-        gather_on_vector(1, ROWS - 1)
-        gather_on_scalar(1, ROWS - 1, *PIECES[1])
-        gather_on_scalar(1, ROWS - 1, *PIECES[2])
-        weave(1, 1, nc.scalar.copy)
-        weave(1, 2, nc.vector.tensor_copy)
-        for i in range(len(PIECES)):
-            quantise(1, i)
-        for c in range(BLOCKS):
-            multiply(1, c)
-            for i, (n0, n1) in enumerate(PRODUCTS[c]):
-                if (c, i) == (0, 0):
-                    nc.vector.tensor_scalar(y[c][:, n0:n1], acc[c][i][:], bias[:, c : c + 1], None, ADD)
-                else:
-                    nc.scalar.activation(y[c][:, n0:n1], acc[c][i][:], IDENTITY, bias=bias[:, c : c + 1])
+        for i in range(2):
+            gather_on_vector(1, ROWS - 1, i * P, (i + 1) * P)
+            gather_on_scalar(1, ROWS - 1, SPLIT + i * P, SPLIT + (i + 1) * P)
+        quantise(1, 0, P)
+        weave(1, 2 * P, 3 * P, nc.scalar.copy)
+        weave(1, 3 * P, 4 * P, nc.vector.tensor_copy)
+        for i in range(1, PIECES):
+            quantise(1, i * P, (i + 1) * P)
+        for c, i in ((0, 0), (1, 0), (0, 1), (1, 1), (0, 2), (0, 3), (1, 2), (1, 3)):
+            multiply(1, c, i)
+            add_bias(c, i)
 
         terms = [held.tile([P, D, V], F32, name=f"terms{c}") for c in range(BLOCKS)]
-        picked = held.tile([P, V], F32, name="picked")
-
-        def add_and_store(c):
+        picked = [held.tile([P, V], F32, name=f"picked{c}") for c in range(BLOCKS)]
+        for c in range(BLOCKS):
+            nc.vector.tensor_tensor(terms[c][:, 0, :], y[c][:].indirect(pos_sb[0][:]), gates[:, 0, :], MULT)
+            nc.scalar.activation(picked[c][:], y[c][:].indirect(pos_sb[1][:]), COPY)
+        for c in range(BLOCKS):
+            nc.vector.tensor_tensor(terms[c][:, 1, :], picked[c][:], gates[:, 1, :], MULT)
+        for c in range(BLOCKS):
             result = held.tile([P, V], F32, name=f"result{c}")
             nc.vector.tensor_tensor(result[:], terms[c][:, 0, :], terms[c][:, 1, :], ADD)
             nc.sync.dma_start(out=out[c * P : (c + 1) * P, :], in_=result[:])
-
-        for c, d in ((0, 0), (0, 1), (1, 0)):
-            nc.vector.tensor_tensor(terms[c][:, d, :], y[c][:].indirect(pos_sb[d][:]), gates[:, d, :], MULT)
-        nc.scalar.activation(picked[:], y[1][:].indirect(pos_sb[1][:]), COPY)
-        nc.vector.tensor_tensor(terms[1][:, 1, :], picked[:], gates[:, 1, :], MULT)
-        add_and_store(0)
-        add_and_store(1)

@@ -22,6 +22,7 @@ BLOCKS = N // P
 LIST_ROWS = 16
 SPLIT = 256
 PIECES = S // P
+VECTOR_CUTS = (((0, SPLIT),), ((0, P), (P, SPLIT)))
 
 FLOPS = 2 * K * S * N + 3 * N * V
 
@@ -36,6 +37,10 @@ def tile_picked_sub_lin_bias_sub_e_kernel(tc, xT, w_words, w_scales, b, gate, of
         pos_sb = [held.tile([P, V // LIST_ROWS], U16, name=f"pos_sb{d}") for d in range(D)]
         rows = [[held.tile([P, T], F32, name=f"row{a}{j}", align_bytes=64) for j in range(ROWS)] for a in range(PASSES)]
         planes = [held.tile([P, ROWS, S - SPLIT], BF16, name=f"planes{a}", align_bytes=64) for a in range(PASSES)]
+        pairs = [
+            [held.tile([P, 2, n1 - n0, 2], BF16, name=f"pairs{a}{n0}", align_bytes=64) for n0, n1 in VECTOR_CUTS[a]]
+            for a in range(PASSES)
+        ]
         grouped = [held.tile([P, ROWS * S], BF16, name=f"grouped{a}", align_bytes=64) for a in range(PASSES)]
         codes = [held.tile([P, S], U32, name=f"codes{a}", align_bytes=64) for a in range(PASSES)]
         scales = [held.tile([P, S], U8, name=f"scales{a}", align_bytes=64) for a in range(PASSES)]
@@ -67,9 +72,16 @@ def tile_picked_sub_lin_bias_sub_e_kernel(tc, xT, w_words, w_scales, b, gate, of
         def entries(n0, n1):
             return offs_sb[:, n0 // LIST_ROWS : n1 // LIST_ROWS]
 
-        def gather_on_vector(a, j, n0, n1):
-            dst = grouped[a][:].rearrange("p (n j) -> p n j", j=ROWS)[:, n0:n1, j]
-            nc.vector.tensor_copy(out=dst, in_=rows[a][j][:].indirect(entries(n0, n1)))
+        def gather_on_vector(a, j):
+            for tile, (n0, n1) in zip(pairs[a], VECTOR_CUTS[a]):
+                nc.vector.tensor_copy(out=tile[:, j // 2, :, j % 2], in_=rows[a][j][:].indirect(entries(n0, n1)))
+
+        def weave_pairs(a):
+            for tile, (n0, n1) in zip(pairs[a], VECTOR_CUTS[a]):
+                nc.vector.tensor_copy(
+                    out=grouped[a][:, ROWS * n0 : ROWS * n1].bitcast(I32).rearrange("p (n u) -> p n u", u=2),
+                    in_=tile[:].rearrange("p u n e -> p u (n e)").bitcast(I32).rearrange("p u n -> p n u"),
+                )
 
         def gather_on_scalar(a, j, n0, n1):
             nc.scalar.activation(planes[a][:, j, n0 - SPLIT : n1 - SPLIT], rows[a][j][:].indirect(entries(n0, n1)), COPY)
@@ -102,10 +114,11 @@ def tile_picked_sub_lin_bias_sub_e_kernel(tc, xT, w_words, w_scales, b, gate, of
                 nc.vector.tensor_scalar(dst, acc[c][i][:], bias[:, c : c + 1], None, ADD)
 
         for j in range(ROWS):
-            gather_on_vector(0, j, 0, SPLIT)
+            gather_on_vector(0, j)
             gather_on_scalar(0, j, SPLIT, S)
         weave(0, SPLIT, S, nc.scalar.copy)
-        gather_on_vector(1, 0, 0, SPLIT)
+        weave_pairs(0)
+        gather_on_vector(1, 0)
         gather_on_scalar(1, 0, SPLIT, S)
         quantise(0, 0, SPLIT)
         quantise(0, SPLIT, S)
@@ -113,11 +126,12 @@ def tile_picked_sub_lin_bias_sub_e_kernel(tc, xT, w_words, w_scales, b, gate, of
             for i in range(PIECES):
                 multiply(0, c, i)
         for j in range(1, ROWS - 1):
-            gather_on_vector(1, j, 0, SPLIT)
+            gather_on_vector(1, j)
             gather_on_scalar(1, j, SPLIT, S)
+        gather_on_vector(1, ROWS - 1)
         for i in range(2):
-            gather_on_vector(1, ROWS - 1, i * P, (i + 1) * P)
             gather_on_scalar(1, ROWS - 1, SPLIT + i * P, SPLIT + (i + 1) * P)
+        weave_pairs(1)
         quantise(1, 0, P)
         weave(1, 2 * P, 3 * P, nc.scalar.copy)
         weave(1, 3 * P, 4 * P, nc.vector.tensor_copy)

@@ -22,7 +22,9 @@ BLOCKS = N // P
 LIST_ROWS = 16
 SPLIT = 256
 PIECES = S // P
+HALF = P // 2
 VECTOR_CUTS = (((0, SPLIT),), ((0, P), (P, SPLIT)))
+SCALAR_CUTS = (((SPLIT, S),), ((SPLIT, SPLIT + P), (SPLIT + P, S)))
 
 FLOPS = 2 * K * S * N + 3 * N * V
 
@@ -41,7 +43,11 @@ def tile_picked_sub_lin_bias_sub_e_kernel(tc, xT, w_words, w_scales, b, gate, of
             [held.tile([P, 2, n1 - n0, 2], BF16, name=f"pairs{a}{n0}", align_bytes=64) for n0, n1 in VECTOR_CUTS[a]]
             for a in range(PASSES)
         ]
-        grouped = [held.tile([P, ROWS * S], BF16, name=f"grouped{a}", align_bytes=64) for a in range(PASSES)]
+        grouped = {
+            (a, n0): held.tile([P, ROWS * (n1 - n0)], BF16, name=f"grouped{a}_{n0}", align_bytes=64)
+            for a in range(PASSES)
+            for n0, n1 in VECTOR_CUTS[a] + SCALAR_CUTS[a]
+        }
         codes = [held.tile([P, S], U32, name=f"codes{a}", align_bytes=64) for a in range(PASSES)]
         scales = [held.tile([P, S], U8, name=f"scales{a}", align_bytes=64) for a in range(PASSES)]
         w_codes = [held.tile([P, N], U32, name=f"w_codes{a}", align_bytes=64) for a in range(PASSES)]
@@ -76,23 +82,28 @@ def tile_picked_sub_lin_bias_sub_e_kernel(tc, xT, w_words, w_scales, b, gate, of
             for tile, (n0, n1) in zip(pairs[a], VECTOR_CUTS[a]):
                 nc.vector.tensor_copy(out=tile[:, j // 2, :, j % 2], in_=rows[a][j][:].indirect(entries(n0, n1)))
 
-        def weave_pairs(a):
-            for tile, (n0, n1) in zip(pairs[a], VECTOR_CUTS[a]):
-                nc.vector.tensor_copy(
-                    out=grouped[a][:, ROWS * n0 : ROWS * n1].bitcast(I32).rearrange("p (n u) -> p n u", u=2),
-                    in_=tile[:].rearrange("p u n e -> p u (n e)").bitcast(I32).rearrange("p u n -> p n u"),
-                )
+        def weave_pairs(a, cut):
+            n0, _ = VECTOR_CUTS[a][cut]
+            nc.vector.tensor_copy(
+                out=grouped[a, n0][:].bitcast(I32).rearrange("p (n u) -> p n u", u=2),
+                in_=pairs[a][cut][:].rearrange("p u n e -> p u (n e)").bitcast(I32).rearrange("p u n -> p n u"),
+            )
 
         def gather_on_scalar(a, j, n0, n1):
             nc.scalar.activation(planes[a][:, j, n0 - SPLIT : n1 - SPLIT], rows[a][j][:].indirect(entries(n0, n1)), COPY)
 
-        def weave(a, n0, n1, copy):
-            src = planes[a][:, :, n0 - SPLIT : n1 - SPLIT].rearrange("p j (c e) -> p c j e", e=4)
-            copy(out=grouped[a][:, ROWS * n0 : ROWS * n1].rearrange("p (c e j) -> p c j e", e=4, j=ROWS), in_=src)
+        def insert_pair(a, u, n0, n1, copy):
+            src = planes[a][:, 2 * u : 2 * u + 2, n0 - SPLIT : n1 - SPLIT].rearrange("p e n -> p n e")
+            first = max(m0 for m0, _ in SCALAR_CUTS[a] if m0 <= n0)
+            dst = grouped[a, first][:].rearrange("p (n j) -> p n j", j=ROWS)
+            copy(out=dst[:, n0 - first : n1 - first, 2 * u : 2 * u + 2], in_=src)
+
+        def gpsimd_copy(out, in_):
+            nc.gpsimd.tensor_scalar(out, in_, 1.0, 0.0, MULT, ADD)
 
         def quantise(a, n0, n1):
             nc.vector.quantize_mx(
-                out=codes[a][:, n0:n1].bitcast(FP8X4), scales=scales[a][:, n0:n1], in_=grouped[a][:, ROWS * n0 : ROWS * n1]
+                out=codes[a][:, n0:n1].bitcast(FP8X4), scales=scales[a][:, n0:n1], in_=grouped[a, n0][:]
             )
 
         def multiply(a, c, i):
@@ -113,11 +124,15 @@ def tile_picked_sub_lin_bias_sub_e_kernel(tc, xT, w_words, w_scales, b, gate, of
             else:
                 nc.vector.tensor_scalar(dst, acc[c][i][:], bias[:, c : c + 1], None, ADD)
 
-        for j in range(ROWS):
+        gather_on_scalar(0, 0, S - HALF, S)
+        gather_on_vector(0, 0)
+        nc.vector.tensor_copy(out=planes[0][:, 0, 0 : S - HALF - SPLIT], in_=rows[0][0][:].indirect(entries(SPLIT, S - HALF)))
+        for j in range(1, ROWS):
             gather_on_vector(0, j)
             gather_on_scalar(0, j, SPLIT, S)
-        weave(0, SPLIT, S, nc.scalar.copy)
-        weave_pairs(0)
+        insert_pair(0, 0, SPLIT, S, gpsimd_copy)
+        insert_pair(0, 1, SPLIT, S, nc.scalar.copy)
+        weave_pairs(0, 0)
         gather_on_vector(1, 0)
         gather_on_scalar(1, 0, SPLIT, S)
         quantise(0, 0, SPLIT)
@@ -128,16 +143,20 @@ def tile_picked_sub_lin_bias_sub_e_kernel(tc, xT, w_words, w_scales, b, gate, of
         for j in range(1, ROWS - 1):
             gather_on_vector(1, j)
             gather_on_scalar(1, j, SPLIT, S)
+        for n0, n1 in SCALAR_CUTS[1]:
+            insert_pair(1, 0, n0, n1, nc.vector.tensor_copy)
         gather_on_vector(1, ROWS - 1)
-        for i in range(2):
-            gather_on_scalar(1, ROWS - 1, SPLIT + i * P, SPLIT + (i + 1) * P)
-        weave_pairs(1)
-        quantise(1, 0, P)
-        weave(1, 2 * P, 3 * P, nc.scalar.copy)
-        weave(1, 3 * P, 4 * P, nc.vector.tensor_copy)
-        for i in range(1, PIECES):
+        halves = ((3 * P, S - HALF), (S - HALF, S))
+        for n0, n1 in ((SPLIT, 3 * P),) + halves:
+            gather_on_scalar(1, ROWS - 1, n0, n1)
+        weave_pairs(1, 0)
+        insert_pair(1, 1, 2 * P, 3 * P, nc.vector.tensor_copy)
+        for n0, n1 in halves:
+            insert_pair(1, 1, n0, n1, nc.scalar.copy)
+        weave_pairs(1, 1)
+        for i in (0, 2, 1, 3):
             quantise(1, i * P, (i + 1) * P)
-        for c, i in ((0, 0), (1, 0), (0, 1), (1, 1), (0, 2), (0, 3), (1, 2), (1, 3)):
+        for c, i in ((0, 0), (1, 0), (0, 2), (1, 2), (0, 1), (0, 3), (1, 1), (1, 3)):
             multiply(1, c, i)
             add_bias(c, i)
 

@@ -23,8 +23,8 @@ LIST_ROWS = 16
 SPLIT = 256
 PIECES = S // P
 HALF = P // 2
+SCALAR_TARGETS = (V, 3 * V // 4)
 VECTOR_CUTS = (((0, SPLIT),), ((0, P), (P, SPLIT)))
-SCALAR_CUTS = (((SPLIT, S),), ((SPLIT, SPLIT + P), (SPLIT + P, S)))
 
 FLOPS = 2 * K * S * N + 3 * N * V
 
@@ -40,13 +40,13 @@ def tile_picked_sub_lin_bias_sub_e_kernel(tc, xT, w_words, w_scales, b, gate, of
         rows = [[held.tile([P, T], F32, name=f"row{a}{j}", align_bytes=64) for j in range(ROWS)] for a in range(PASSES)]
         planes = [held.tile([P, ROWS, S - SPLIT], BF16, name=f"planes{a}", align_bytes=64) for a in range(PASSES)]
         pairs = [
-            [held.tile([P, 2, n1 - n0, 2], BF16, name=f"pairs{a}{n0}", align_bytes=64) for n0, n1 in VECTOR_CUTS[a]]
-            for a in range(PASSES)
+            held.tile([P, len(cuts), 2, SPLIT // len(cuts), 2], BF16, name=f"pairs{a}", align_bytes=64)
+            for a, cuts in enumerate(VECTOR_CUTS)
         ]
         grouped = {
             (a, n0): held.tile([P, ROWS * (n1 - n0)], BF16, name=f"grouped{a}_{n0}", align_bytes=64)
             for a in range(PASSES)
-            for n0, n1 in VECTOR_CUTS[a] + SCALAR_CUTS[a]
+            for n0, n1 in VECTOR_CUTS[a] + ((SPLIT, S),)
         }
         codes = [held.tile([P, S], U32, name=f"codes{a}", align_bytes=64) for a in range(PASSES)]
         scales = [held.tile([P, S], U8, name=f"scales{a}", align_bytes=64) for a in range(PASSES)]
@@ -78,15 +78,17 @@ def tile_picked_sub_lin_bias_sub_e_kernel(tc, xT, w_words, w_scales, b, gate, of
         def entries(n0, n1):
             return offs_sb[:, n0 // LIST_ROWS : n1 // LIST_ROWS]
 
-        def gather_on_vector(a, j):
-            for tile, (n0, n1) in zip(pairs[a], VECTOR_CUTS[a]):
-                nc.vector.tensor_copy(out=tile[:, j // 2, :, j % 2], in_=rows[a][j][:].indirect(entries(n0, n1)))
+        def gather_on_vector(a, j, cut0=0, cut1=None):
+            cut1 = cut1 or len(VECTOR_CUTS[a])
+            cuts = VECTOR_CUTS[a][cut0:cut1]
+            dst = pairs[a][:, cut0:cut1, j // 2, :, j % 2]
+            nc.vector.tensor_copy(out=dst, in_=rows[a][j][:].indirect(entries(cuts[0][0], cuts[-1][1])))
 
         def weave_pairs(a, cut):
             n0, _ = VECTOR_CUTS[a][cut]
             nc.vector.tensor_copy(
                 out=grouped[a, n0][:].bitcast(I32).rearrange("p (n u) -> p n u", u=2),
-                in_=pairs[a][cut][:].rearrange("p u n e -> p u (n e)").bitcast(I32).rearrange("p u n -> p n u"),
+                in_=pairs[a][:, cut].rearrange("p u n e -> p u (n e)").bitcast(I32).rearrange("p u n -> p n u"),
             )
 
         def gather_on_scalar(a, j, n0, n1):
@@ -94,17 +96,16 @@ def tile_picked_sub_lin_bias_sub_e_kernel(tc, xT, w_words, w_scales, b, gate, of
 
         def insert_pair(a, u, n0, n1, copy):
             src = planes[a][:, 2 * u : 2 * u + 2, n0 - SPLIT : n1 - SPLIT].rearrange("p e n -> p n e")
-            first = max(m0 for m0, _ in SCALAR_CUTS[a] if m0 <= n0)
-            dst = grouped[a, first][:].rearrange("p (n j) -> p n j", j=ROWS)
-            copy(out=dst[:, n0 - first : n1 - first, 2 * u : 2 * u + 2], in_=src)
+            dst = grouped[a, SPLIT][:].rearrange("p (n j) -> p n j", j=ROWS)
+            copy(out=dst[:, n0 - SPLIT : n1 - SPLIT, 2 * u : 2 * u + 2], in_=src)
 
         def gpsimd_copy(out, in_):
             nc.gpsimd.tensor_scalar(out, in_, 1.0, 0.0, MULT, ADD)
 
         def quantise(a, n0, n1):
-            nc.vector.quantize_mx(
-                out=codes[a][:, n0:n1].bitcast(FP8X4), scales=scales[a][:, n0:n1], in_=grouped[a, n0][:]
-            )
+            first = min(n0, SPLIT)
+            src = grouped[a, first][:, ROWS * (n0 - first) : ROWS * (n1 - first)]
+            nc.vector.quantize_mx(out=codes[a][:, n0:n1].bitcast(FP8X4), scales=scales[a][:, n0:n1], in_=src)
 
         def multiply(a, c, i):
             nc.tensor.matmul_mx(
@@ -119,7 +120,7 @@ def tile_picked_sub_lin_bias_sub_e_kernel(tc, xT, w_words, w_scales, b, gate, of
 
         def add_bias(c, i):
             dst = y[c][:, i * P : (i + 1) * P]
-            if c == 0:
+            if (c, i) not in ((1, 0), (1, 2)):
                 nc.scalar.activation(dst, acc[c][i][:], IDENTITY, bias=bias[:, c : c + 1])
             else:
                 nc.vector.tensor_scalar(dst, acc[c][i][:], bias[:, c : c + 1], None, ADD)
@@ -143,9 +144,9 @@ def tile_picked_sub_lin_bias_sub_e_kernel(tc, xT, w_words, w_scales, b, gate, of
         for j in range(1, ROWS - 1):
             gather_on_vector(1, j)
             gather_on_scalar(1, j, SPLIT, S)
-        for n0, n1 in SCALAR_CUTS[1]:
-            insert_pair(1, 0, n0, n1, nc.vector.tensor_copy)
-        gather_on_vector(1, ROWS - 1)
+        insert_pair(1, 0, SPLIT, S, nc.vector.tensor_copy)
+        for cut in range(2):
+            gather_on_vector(1, ROWS - 1, cut, cut + 1)
         halves = ((3 * P, S - HALF), (S - HALF, S))
         for n0, n1 in ((SPLIT, 3 * P),) + halves:
             gather_on_scalar(1, ROWS - 1, n0, n1)
@@ -156,17 +157,19 @@ def tile_picked_sub_lin_bias_sub_e_kernel(tc, xT, w_words, w_scales, b, gate, of
         weave_pairs(1, 1)
         for i in (0, 2, 1, 3):
             quantise(1, i * P, (i + 1) * P)
-        for c, i in ((0, 0), (1, 0), (0, 2), (1, 2), (0, 1), (0, 3), (1, 1), (1, 3)):
+        for c, i in ((0, 0), (1, 0), (0, 2), (0, 1), (0, 3), (1, 2), (1, 1), (1, 3)):
             multiply(1, c, i)
             add_bias(c, i)
 
         terms = [held.tile([P, D, V], F32, name=f"terms{c}") for c in range(BLOCKS)]
-        picked = [held.tile([P, V], F32, name=f"picked{c}") for c in range(BLOCKS)]
+        picked = [held.tile([P, v1], F32, name=f"picked{c}") for c, v1 in enumerate(SCALAR_TARGETS)]
         for c in range(BLOCKS):
             nc.vector.tensor_tensor(terms[c][:, 0, :], y[c][:].indirect(pos_sb[0][:]), gates[:, 0, :], MULT)
-            nc.scalar.activation(picked[c][:], y[c][:].indirect(pos_sb[1][:]), COPY)
-        for c in range(BLOCKS):
-            nc.vector.tensor_tensor(terms[c][:, 1, :], picked[c][:], gates[:, 1, :], MULT)
+            nc.scalar.activation(picked[c][:], y[c][:].indirect(pos_sb[1][:, 0 : SCALAR_TARGETS[c] // LIST_ROWS]), COPY)
+        v0 = SCALAR_TARGETS[1]
+        nc.vector.tensor_tensor(terms[0][:, 1, :], picked[0][:], gates[:, 1, :], MULT)
+        nc.vector.tensor_tensor(terms[1][:, 1, v0:V], y[1][:].indirect(pos_sb[1][:, v0 // LIST_ROWS :]), gates[:, 1, v0:V], MULT)
+        nc.vector.tensor_tensor(terms[1][:, 1, 0:v0], picked[1][:], gates[:, 1, 0:v0], MULT)
         for c in range(BLOCKS):
             result = held.tile([P, V], F32, name=f"result{c}")
             nc.vector.tensor_tensor(result[:], terms[c][:, 0, :], terms[c][:, 1, :], ADD)

@@ -37,7 +37,7 @@ def tile_picked_sub_lin_bias_sub_e_kernel(tc, xT, w_words, w_scales, b, gate, of
 
         offs_sb = held.tile([P, S // LIST_ROWS], U16, name="offs_sb")
         pos_sb = [held.tile([P, V // LIST_ROWS], U16, name=f"pos_sb{d}") for d in range(D)]
-        rows = [[held.tile([P, T], F32, name=f"row{a}{j}", align_bytes=64) for j in range(ROWS)] for a in range(PASSES)]
+        rows = [[held.tile([P, T], F32, name=f"row{a}{j}", align_bytes=256) for j in range(ROWS)] for a in range(PASSES)]
         planes = [held.tile([P, ROWS, S - SPLIT], BF16, name=f"planes{a}", align_bytes=64) for a in range(PASSES)]
         pairs = [
             held.tile([P, len(cuts), 2, SPLIT // len(cuts), 2], BF16, name=f"pairs{a}", align_bytes=64)
@@ -49,10 +49,10 @@ def tile_picked_sub_lin_bias_sub_e_kernel(tc, xT, w_words, w_scales, b, gate, of
             for n0, n1 in VECTOR_CUTS[a] + ((SPLIT, S),)
         }
         codes = [held.tile([P, S], U32, name=f"codes{a}", align_bytes=64) for a in range(PASSES)]
-        scales = [held.tile([P, S], U8, name=f"scales{a}", align_bytes=64) for a in range(PASSES)]
-        w_codes = [held.tile([P, N], U32, name=f"w_codes{a}", align_bytes=64) for a in range(PASSES)]
+        scales = [held.tile([P, S], U8, name=f"scales{a}", align_bytes=256) for a in range(PASSES)]
+        w_codes = [held.tile([P, N], U32, name=f"w_codes{a}", align_bytes=256) for a in range(PASSES)]
         bias = held.tile([P, BLOCKS], F32, name="bias")
-        gates = held.tile([P, D, V], F32, name="gates")
+        gates = held.tile([P, D, V], F32, name="gates", align_bytes=256)
         y = [held.tile([P, S], F32, name=f"y{c}") for c in range(BLOCKS)]
 
         scale_rows = w_scales.rearrange("a (q r) n -> q a r n", r=4).bitcast(I32)
@@ -171,6 +171,6 @@ def tile_picked_sub_lin_bias_sub_e_kernel(tc, xT, w_words, w_scales, b, gate, of
         nc.vector.tensor_tensor(terms[1][:, 1, v0:V], y[1][:].indirect(pos_sb[1][:, v0 // LIST_ROWS :]), gates[:, 1, v0:V], MULT)
         nc.vector.tensor_tensor(terms[1][:, 1, 0:v0], picked[1][:], gates[:, 1, 0:v0], MULT)
         for c in range(BLOCKS):
-            result = held.tile([P, V], F32, name=f"result{c}")
+            result = held.tile([P, V], F32, name=f"result{c}", align_bytes=256)
             nc.vector.tensor_tensor(result[:], terms[c][:, 0, :], terms[c][:, 1, :], ADD)
             nc.sync.dma_start(out=out[c * P : (c + 1) * P, :], in_=result[:])

@@ -66,12 +66,13 @@ def tile_picked_sub_lin_bias_sub_e_kernel(tc, xT, w_words, w_scales, b, gate, of
                         rows_q = scales[0][32 * q + 4 : 32 * q + 4 + 4 * PASSES, 0:N]
                         nc.scalar.dma_start(out=rows_q.bitcast(I32), in_=scale_rows[q])
         words = w_words.rearrange("a p n r -> a p (n r)").bitcast(I32)
-        for a, m0, m1 in ((0, 0, P), (0, P, N), (1, 0, N)):
+        for a, m0, m1 in ((0, 0, P), (0, P, N), (1, 0, P), (1, P, N)):
             nc.sync.dma_start(out=w_codes[a][:, m0:m1].bitcast(I32), in_=words[a][:, m0:m1])
         nc.sync.dma_start(out=bias[:], in_=b.rearrange("(c p) o -> p (c o)", c=BLOCKS))
         nc.sync.dma_start(pos_sb[0][:], pos1)
+        nc.sync.dma_start(out=gates[:, 0, :], in_=gate[0, 0:P])
         nc.sync.dma_start(pos_sb[1][:], pos2)
-        nc.sync.dma_start(out=gates[:], in_=gate.rearrange("d m v -> m d v")[0:P])
+        nc.sync.dma_start(out=gates[:, 1, :], in_=gate[1, 0:P])
 
         acc = [[psum.tile([P, P], F32, name=f"acc{c}{i}") for i in range(PIECES)] for c in range(BLOCKS)]
 

@@ -20,11 +20,9 @@ PASSES = K // 512
 ROWS = 4
 BLOCKS = N // P
 LIST_ROWS = 16
-SPLIT = 256
 PIECES = S // P
-HALF = P // 2
+VECTOR_ENTRIES = (320, 192)
 SCALAR_TARGETS = (V, 3 * V // 4)
-VECTOR_CUTS = (((0, SPLIT),), ((0, P), (P, SPLIT)))
 
 FLOPS = 2 * K * S * N + 3 * N * V
 
@@ -38,16 +36,7 @@ def tile_picked_sub_lin_bias_sub_e_kernel(tc, xT, w_words, w_scales, b, gate, of
         offs_sb = held.tile([P, S // LIST_ROWS], U16, name="offs_sb")
         pos_sb = [held.tile([P, V // LIST_ROWS], U16, name=f"pos_sb{d}") for d in range(D)]
         rows = [[held.tile([P, T], F32, name=f"row{a}{j}", align_bytes=256) for j in range(ROWS)] for a in range(PASSES)]
-        planes = [held.tile([P, ROWS, S - SPLIT], BF16, name=f"planes{a}", align_bytes=64) for a in range(PASSES)]
-        pairs = [
-            held.tile([P, len(cuts), 2, SPLIT // len(cuts), 2], BF16, name=f"pairs{a}", align_bytes=64)
-            for a, cuts in enumerate(VECTOR_CUTS)
-        ]
-        grouped = {
-            (a, n0): held.tile([P, ROWS * (n1 - n0)], BF16, name=f"grouped{a}_{n0}", align_bytes=64)
-            for a in range(PASSES)
-            for n0, n1 in VECTOR_CUTS[a] + ((SPLIT, S),)
-        }
+        grouped = [held.tile([P, ROWS * S], BF16, name=f"grouped{a}", align_bytes=64) for a in range(PASSES)]
         codes = [held.tile([P, S], U32, name=f"codes{a}", align_bytes=64) for a in range(PASSES)]
         scales = [held.tile([P, S], U8, name=f"scales{a}", align_bytes=256) for a in range(PASSES)]
         w_codes = [held.tile([P, N], U32, name=f"w_codes{a}", align_bytes=256) for a in range(PASSES)]
@@ -76,36 +65,21 @@ def tile_picked_sub_lin_bias_sub_e_kernel(tc, xT, w_words, w_scales, b, gate, of
 
         acc = [[psum.tile([P, P], F32, name=f"acc{c}{i}") for i in range(PIECES)] for c in range(BLOCKS)]
 
-        def entries(n0, n1):
-            return offs_sb[:, n0 // LIST_ROWS : n1 // LIST_ROWS]
+        def picked_row(a, j, n0, n1):
+            return rows[a][j][:].indirect(offs_sb[:, n0 // LIST_ROWS : n1 // LIST_ROWS])
 
-        def gather_on_vector(a, j, cut0=0, cut1=None):
-            cut1 = cut1 or len(VECTOR_CUTS[a])
-            cuts = VECTOR_CUTS[a][cut0:cut1]
-            dst = pairs[a][:, cut0:cut1, j // 2, :, j % 2]
-            nc.vector.tensor_copy(out=dst, in_=rows[a][j][:].indirect(entries(cuts[0][0], cuts[-1][1])))
+        def slot(a, j, n0, n1):
+            return grouped[a][:].rearrange("p (n j) -> p n j", j=ROWS)[:, n0:n1, j]
 
-        def weave_pairs(a, cut):
-            n0, _ = VECTOR_CUTS[a][cut]
-            nc.vector.tensor_copy(
-                out=grouped[a, n0][:].bitcast(I32).rearrange("p (n u) -> p n u", u=2),
-                in_=pairs[a][:, cut].rearrange("p u n e -> p u (n e)").bitcast(I32).rearrange("p u n -> p n u"),
-            )
+        def gather_on_vector(a, j):
+            n1 = VECTOR_ENTRIES[a]
+            nc.vector.tensor_copy(out=slot(a, j, 0, n1), in_=picked_row(a, j, 0, n1))
 
         def gather_on_scalar(a, j, n0, n1):
-            nc.scalar.activation(planes[a][:, j, n0 - SPLIT : n1 - SPLIT], rows[a][j][:].indirect(entries(n0, n1)), COPY)
-
-        def insert_pair(a, u, n0, n1, copy):
-            src = planes[a][:, 2 * u : 2 * u + 2, n0 - SPLIT : n1 - SPLIT].rearrange("p e n -> p n e")
-            dst = grouped[a, SPLIT][:].rearrange("p (n j) -> p n j", j=ROWS)
-            copy(out=dst[:, n0 - SPLIT : n1 - SPLIT, 2 * u : 2 * u + 2], in_=src)
-
-        def gpsimd_copy(out, in_):
-            nc.gpsimd.tensor_scalar(out, in_, 1.0, 0.0, MULT, ADD)
+            nc.scalar.activation(slot(a, j, n0, n1), picked_row(a, j, n0, n1), COPY)
 
         def quantise(a, n0, n1):
-            first = min(n0, SPLIT)
-            src = grouped[a, first][:, ROWS * (n0 - first) : ROWS * (n1 - first)]
+            src = grouped[a][:, ROWS * n0 : ROWS * n1]
             nc.vector.quantize_mx(out=codes[a][:, n0:n1].bitcast(FP8X4), scales=scales[a][:, n0:n1], in_=src)
 
         def multiply(a, c, i):
@@ -121,44 +95,29 @@ def tile_picked_sub_lin_bias_sub_e_kernel(tc, xT, w_words, w_scales, b, gate, of
 
         def add_bias(c, i):
             dst = y[c][:, i * P : (i + 1) * P]
-            if (c, i) not in ((1, 0), (1, 2)):
+            if (c, i) not in ((1, 2), (1, 1)):
                 nc.scalar.activation(dst, acc[c][i][:], IDENTITY, bias=bias[:, c : c + 1])
             else:
                 nc.vector.tensor_scalar(dst, acc[c][i][:], bias[:, c : c + 1], None, ADD)
 
-        gather_on_scalar(0, 0, S - HALF, S)
-        gather_on_vector(0, 0)
-        nc.vector.tensor_copy(out=planes[0][:, 0, 0 : S - HALF - SPLIT], in_=rows[0][0][:].indirect(entries(SPLIT, S - HALF)))
-        for j in range(1, ROWS):
+        for j in range(ROWS):
             gather_on_vector(0, j)
-            gather_on_scalar(0, j, SPLIT, S)
-        insert_pair(0, 0, SPLIT, S, gpsimd_copy)
-        insert_pair(0, 1, SPLIT, S, nc.scalar.copy)
-        weave_pairs(0, 0)
+            gather_on_scalar(0, j, VECTOR_ENTRIES[0], S)
         gather_on_vector(1, 0)
-        gather_on_scalar(1, 0, SPLIT, S)
-        quantise(0, 0, SPLIT)
-        quantise(0, SPLIT, S)
+        gather_on_scalar(1, 0, VECTOR_ENTRIES[1], S)
+        quantise(0, 0, S)
         for c in range(BLOCKS):
             for i in range(PIECES):
                 multiply(0, c, i)
         for j in range(1, ROWS - 1):
             gather_on_vector(1, j)
-            gather_on_scalar(1, j, SPLIT, S)
-        insert_pair(1, 0, SPLIT, S, nc.vector.tensor_copy)
-        for cut in range(2):
-            gather_on_vector(1, ROWS - 1, cut, cut + 1)
-        halves = ((3 * P, S - HALF), (S - HALF, S))
-        for n0, n1 in ((SPLIT, 3 * P),) + halves:
+            gather_on_scalar(1, j, VECTOR_ENTRIES[1], S)
+        gather_on_vector(1, ROWS - 1)
+        for n0, n1 in ((2 * P, 3 * P), (VECTOR_ENTRIES[1], 2 * P), (3 * P, S)):
             gather_on_scalar(1, ROWS - 1, n0, n1)
-        weave_pairs(1, 0)
-        insert_pair(1, 1, 2 * P, 3 * P, nc.vector.tensor_copy)
-        for n0, n1 in halves:
-            insert_pair(1, 1, n0, n1, nc.scalar.copy)
-        weave_pairs(1, 1)
-        for i in (0, 2, 1, 3):
+        for i in (2, 0, 1, 3):
             quantise(1, i * P, (i + 1) * P)
-        for c, i in ((0, 0), (1, 0), (0, 2), (0, 1), (0, 3), (1, 2), (1, 1), (1, 3)):
+        for c, i in ((0, 2), (0, 0), (1, 2), (0, 1), (0, 3), (1, 0), (1, 1), (1, 3)):
             multiply(1, c, i)
             add_bias(c, i)
 

@@ -22,7 +22,7 @@ BLOCKS = N // P
 LIST_ROWS = 16
 PIECES = S // P
 VECTOR_ENTRIES = (320, 192)
-SCALAR_TARGETS = (V, 3 * V // 4)
+LAST_TARGETS = 64
 
 FLOPS = 2 * K * S * N + 3 * N * V
 
@@ -122,14 +122,13 @@ def tile_picked_sub_lin_bias_sub_e_kernel(tc, xT, w_words, w_scales, b, gate, of
             add_bias(c, i)
 
         terms = [held.tile([P, D, V], F32, name=f"terms{c}") for c in range(BLOCKS)]
-        picked = [held.tile([P, v1], F32, name=f"picked{c}") for c, v1 in enumerate(SCALAR_TARGETS)]
+        picked = [held.tile([P, V], F32, name=f"picked{c}") for c in range(BLOCKS)]
         for c in range(BLOCKS):
             nc.vector.tensor_tensor(terms[c][:, 0, :], y[c][:].indirect(pos_sb[0][:]), gates[:, 0, :], MULT)
-            nc.scalar.activation(picked[c][:], y[c][:].indirect(pos_sb[1][:, 0 : SCALAR_TARGETS[c] // LIST_ROWS]), COPY)
-        v0 = SCALAR_TARGETS[1]
-        nc.vector.tensor_tensor(terms[0][:, 1, :], picked[0][:], gates[:, 1, :], MULT)
-        nc.vector.tensor_tensor(terms[1][:, 1, v0:V], y[1][:].indirect(pos_sb[1][:, v0 // LIST_ROWS :]), gates[:, 1, v0:V], MULT)
-        nc.vector.tensor_tensor(terms[1][:, 1, 0:v0], picked[1][:], gates[:, 1, 0:v0], MULT)
+        for c, v0, v1 in ((0, 0, V), (1, 0, V - LAST_TARGETS), (1, V - LAST_TARGETS, V)):
+            places = pos_sb[1][:, v0 // LIST_ROWS : v1 // LIST_ROWS]
+            nc.scalar.activation(picked[c][:, v0:v1], y[c][:].indirect(places), COPY)
+            nc.vector.tensor_tensor(terms[c][:, 1, v0:v1], picked[c][:, v0:v1], gates[:, 1, v0:v1], MULT)
         for c in range(BLOCKS):
             result = held.tile([P, V], F32, name=f"result{c}", align_bytes=256)
             nc.vector.tensor_tensor(result[:], terms[c][:, 0, :], terms[c][:, 1, :], ADD)

@@ -95,7 +95,7 @@ def tile_picked_sub_lin_bias_sub_e_kernel(tc, xT, w_words, w_scales, b, gate, of
 
         def add_bias(c, i):
             dst = y[c][:, i * P : (i + 1) * P]
-            if (c, i) not in ((1, 2), (1, 1)):
+            if (c, i) not in ((1, 2), (1, 0)):
                 nc.scalar.activation(dst, acc[c][i][:], IDENTITY, bias=bias[:, c : c + 1])
             else:
                 nc.vector.tensor_scalar(dst, acc[c][i][:], bias[:, c : c + 1], None, ADD)
@@ -113,13 +113,15 @@ def tile_picked_sub_lin_bias_sub_e_kernel(tc, xT, w_words, w_scales, b, gate, of
             gather_on_vector(1, j)
             gather_on_scalar(1, j, VECTOR_ENTRIES[1], S)
         gather_on_vector(1, ROWS - 1)
-        for n0, n1 in ((2 * P, 3 * P), (VECTOR_ENTRIES[1], 2 * P), (3 * P, S)):
+        halves = ((3 * P, S - P // 2), (S - P // 2, S))
+        for n0, n1 in ((2 * P, 3 * P), (VECTOR_ENTRIES[1], 2 * P)) + halves:
             gather_on_scalar(1, ROWS - 1, n0, n1)
-        for i in (2, 0, 1, 3):
-            quantise(1, i * P, (i + 1) * P)
-        for c, i in ((0, 2), (0, 0), (1, 2), (0, 1), (0, 3), (1, 0), (1, 1), (1, 3)):
-            multiply(1, c, i)
-            add_bias(c, i)
+        for n0, n1 in ((2 * P, 3 * P), (0, P), (P, 2 * P)) + halves:
+            quantise(1, n0, n1)
+        for c in range(BLOCKS):
+            for i in (2, 0, 1, 3):
+                multiply(1, c, i)
+                add_bias(c, i)
 
         terms = [held.tile([P, D, V], F32, name=f"terms{c}") for c in range(BLOCKS)]
         picked = [held.tile([P, V], F32, name=f"picked{c}") for c in range(BLOCKS)]

from contextlib import ExitStack

import concourse.mybir as mybir

F32 = mybir.dt.float32
BF16 = mybir.dt.bfloat16
U32 = mybir.dt.uint32
I32 = mybir.dt.int32
U16 = mybir.dt.uint16
U8 = mybir.dt.uint8
FP8X4 = mybir.dt.float8_e4m3fn_x4
MULT = mybir.AluOpType.mult
ADD = mybir.AluOpType.add
COPY = mybir.ActivationFunctionType.Copy
IDENTITY = mybir.ActivationFunctionType.Identity

P = 128
K, T, S, V, N, D = 1024, 1024, 512, 256, 256, 2
PASSES = K // 512
ROWS = 4
BLOCKS = N // P
LIST_ROWS = 16
PIECES = S // P
VECTOR_ENTRIES = (320, 192)
LAST_TARGETS = 64

FLOPS = 2 * K * S * N + 3 * N * V


def tile_picked_sub_lin_bias_sub_e_kernel(tc, xT, w_words, w_scales, b, gate, offs, pos1, pos2, out):
    nc = tc.nc
    with ExitStack() as ctx:
        held = ctx.enter_context(tc.tile_pool(name="held", bufs=1))
        psum = ctx.enter_context(tc.psum_pool(name="psum", bufs=1))

        offs_sb = held.tile([P, S // LIST_ROWS], U16, name="offs_sb")
        pos_sb = [held.tile([P, V // LIST_ROWS], U16, name=f"pos_sb{d}") for d in range(D)]
        rows = [[held.tile([P, T], F32, name=f"row{a}{j}", align_bytes=256) for j in range(ROWS)] for a in range(PASSES)]
        grouped = [held.tile([P, ROWS * S], BF16, name=f"grouped{a}", align_bytes=64) for a in range(PASSES)]
        codes = [held.tile([P, S], U32, name=f"codes{a}", align_bytes=64) for a in range(PASSES)]
        scales = [held.tile([P, S], U8, name=f"scales{a}", align_bytes=256) for a in range(PASSES)]
        w_codes = [held.tile([P, N], U32, name=f"w_codes{a}", align_bytes=256) for a in range(PASSES)]
        bias = held.tile([P, BLOCKS], F32, name="bias")
        gates = held.tile([P, D, V], F32, name="gates", align_bytes=256)
        y = [held.tile([P, S], F32, name=f"y{c}") for c in range(BLOCKS)]

        scale_rows = w_scales.rearrange("a (q r) n -> q a r n", r=4).bitcast(I32)
        x_rows = xT.rearrange("(a p j) t -> a j p t", a=PASSES, j=ROWS)
        for a in range(PASSES):
            for j in range(ROWS):
                nc.sync.dma_start(out=rows[a][j][:], in_=x_rows[a, j])
                if (a, j) == (0, 0):
                    nc.sync.dma_start(offs_sb[:], offs)
                    for q in range(4):
                        rows_q = scales[0][32 * q + 4 : 32 * q + 4 + 4 * PASSES, 0:N]
                        nc.scalar.dma_start(out=rows_q.bitcast(I32), in_=scale_rows[q])
        words = w_words.rearrange("a p n r -> a p (n r)").bitcast(I32)
        for a, m0, m1 in ((0, 0, P), (0, P, N), (1, 0, P), (1, P, N)):
            nc.sync.dma_start(out=w_codes[a][:, m0:m1].bitcast(I32), in_=words[a][:, m0:m1])
        nc.sync.dma_start(out=bias[:], in_=b.rearrange("(c p) o -> p (c o)", c=BLOCKS))
        nc.sync.dma_start(pos_sb[0][:], pos1)
        nc.sync.dma_start(out=gates[:, 0, :], in_=gate[0, 0:P])
        nc.sync.dma_start(pos_sb[1][:], pos2)
        nc.sync.dma_start(out=gates[:, 1, :], in_=gate[1, 0:P])

        acc = [[psum.tile([P, P], F32, name=f"acc{c}{i}") for i in range(PIECES)] for c in range(BLOCKS)]

        def picked_row(a, j, n0, n1):
            return rows[a][j][:].indirect(offs_sb[:, n0 // LIST_ROWS : n1 // LIST_ROWS])

        def slot(a, j, n0, n1):
            return grouped[a][:].rearrange("p (n j) -> p n j", j=ROWS)[:, n0:n1, j]

        def gather_on_vector(a, j):
            n1 = VECTOR_ENTRIES[a]
            nc.vector.tensor_copy(out=slot(a, j, 0, n1), in_=picked_row(a, j, 0, n1))

        def gather_on_scalar(a, j, n0, n1):
            nc.scalar.activation(slot(a, j, n0, n1), picked_row(a, j, n0, n1), COPY)

        def quantise(a, n0, n1):
            src = grouped[a][:, ROWS * n0 : ROWS * n1]
            nc.vector.quantize_mx(out=codes[a][:, n0:n1].bitcast(FP8X4), scales=scales[a][:, n0:n1], in_=src)

        def multiply(a, c, i):
            nc.tensor.matmul_mx(
                out=acc[c][i][:],
                lhsT=w_codes[a][:, c * P : (c + 1) * P].bitcast(FP8X4),
                lhsT_scale=scales[0][4 + 4 * a :, c * P : (c + 1) * P],
                rhs=codes[a][:, i * P : (i + 1) * P].bitcast(FP8X4),
                rhs_scale=scales[a][:, i * P : (i + 1) * P],
                start=(a == 0),
                stop=(a == PASSES - 1),
            )

        def add_bias(c, i):
            dst = y[c][:, i * P : (i + 1) * P]
            if (c, i) not in ((1, 2), (1, 0)):
                nc.scalar.activation(dst, acc[c][i][:], IDENTITY, bias=bias[:, c : c + 1])
            else:
                nc.vector.tensor_scalar(dst, acc[c][i][:], bias[:, c : c + 1], None, ADD)

        for j in range(ROWS):
            gather_on_vector(0, j)
            gather_on_scalar(0, j, VECTOR_ENTRIES[0], S)
        gather_on_vector(1, 0)
        gather_on_scalar(1, 0, VECTOR_ENTRIES[1], S)
        quantise(0, 0, S)
        for c in range(BLOCKS):
            for i in range(PIECES):
                multiply(0, c, i)
        for j in range(1, ROWS - 1):
            gather_on_vector(1, j)
            gather_on_scalar(1, j, VECTOR_ENTRIES[1], S)
        gather_on_vector(1, ROWS - 1)
        halves = ((3 * P, S - P // 2), (S - P // 2, S))
        for n0, n1 in ((2 * P, 3 * P), (VECTOR_ENTRIES[1], 2 * P)) + halves:
            gather_on_scalar(1, ROWS - 1, n0, n1)
        for n0, n1 in ((2 * P, 3 * P), (0, P), (P, 2 * P)) + halves:
            quantise(1, n0, n1)
        for c in range(BLOCKS):
            for i in (2, 0, 1, 3):
                multiply(1, c, i)
                add_bias(c, i)

        terms = [held.tile([P, D, V], F32, name=f"terms{c}") for c in range(BLOCKS)]
        picked = [held.tile([P, V], F32, name=f"picked{c}") for c in range(BLOCKS)]
        for c in range(BLOCKS):
            nc.vector.tensor_tensor(terms[c][:, 0, :], y[c][:].indirect(pos_sb[0][:]), gates[:, 0, :], MULT)
        for c, v0, v1 in ((0, 0, V), (1, 0, V - LAST_TARGETS), (1, V - LAST_TARGETS, V)):
            places = pos_sb[1][:, v0 // LIST_ROWS : v1 // LIST_ROWS]
            nc.scalar.activation(picked[c][:, v0:v1], y[c][:].indirect(places), COPY)
            nc.vector.tensor_tensor(terms[c][:, 1, v0:v1], picked[c][:, v0:v1], gates[:, 1, v0:v1], MULT)
        for c in range(BLOCKS):
            result = held.tile([P, V], F32, name=f"result{c}", align_bytes=256)
            nc.vector.tensor_tensor(result[:], terms[c][:, 0, :], terms[c][:, 1, :], ADD)
            nc.sync.dma_start(out=out[c * P : (c + 1) * P, :], in_=result[:])
